import numpy as np
import ml_dtypes


def mxq(x, axis, fmt="e4m3"):
    dtype, down = {"e4m3": (ml_dtypes.float8_e4m3fn, 7), "e5m2": (ml_dtypes.float8_e5m2, 14)}[fmt]
    v = np.moveaxis(np.asarray(x, np.float32).astype(ml_dtypes.bfloat16).astype(np.float64), axis, -1)
    blocks = v.reshape(v.shape[:-1] + (-1, 32))
    amax = np.abs(blocks).max(-1, keepdims=True)
    byte = np.maximum(np.where(amax > 0, np.frexp(amax)[1] - 1 + 127, 0) - down, 1)
    scale = np.exp2(byte - 127.0)
    codes = (blocks / scale).astype(np.float32).astype(dtype).astype(np.float64)
    return np.moveaxis((codes * scale).reshape(v.shape), -1, axis)


WIDE = False


def mx_kscale(k):
    if not WIDE:
        return np.ones(k)
    levels = np.array([10, -10, 5, -5, 0])
    if k % 512:
        return np.exp2(np.random.permutation(np.resize(levels, k // 32))).repeat(32)
    a = np.empty((k // 512, 16))
    for p in range(k // 512):
        a[p, :8] = np.random.permutation(np.resize(levels, 8))
        for g in range(8):
            far = levels[np.abs(levels - a[p, g]) >= 10]
            a[p, g + 8] = far[np.random.randint(len(far))]
    return np.exp2(a.ravel()).repeat(32)


def f64(x):
    return np.asarray(x).astype(np.float64)


def striped(idx):
    return np.tile(idx.reshape(-1, 16).T, (8, 1)).astype(np.uint16)


def unstriped(offs):
    return offs[:16].T.reshape(-1).astype(np.int64)


def pack_weight(w):
    k, n = w.shape
    w = f64(np.asarray(w, np.float32).astype(ml_dtypes.bfloat16)).reshape(k // 32, 32, n)
    amax = np.abs(w).max(1)
    byte = np.clip(np.where(amax > 0, np.frexp(amax)[1] - 1 + 127 - 7, 1), 1, 254)
    scaled = (w * np.exp2(127.0 - byte)[:, None, :]).reshape(k, n).astype(np.float32)
    words = np.ascontiguousarray(scaled.reshape(k // 512, 128, 4, n).transpose(0, 1, 3, 2)).astype(ml_dtypes.float8_e4m3fn).view(np.uint8)
    return words, np.ascontiguousarray(byte.astype(np.uint8).reshape(k // 512, 16, n))


def unpack_weight(words, scales):
    g, p, n, _ = words.shape
    vals = np.ascontiguousarray(words).view(ml_dtypes.float8_e4m3fn).astype(np.float64) * np.repeat(np.exp2(scales.astype(np.float64) - 127.0), 8, axis=1)[..., None]
    return vals.transpose(0, 1, 3, 2).reshape(g * 512, n)

def planes(y):
    n, m = y.shape
    v = y.astype(np.float32).astype(ml_dtypes.bfloat16).astype(np.float64).reshape(n // 32, 32, m)
    top = np.abs(v).max(1)
    byte = np.clip(np.where(top > 0, np.frexp(top)[1] - 1 + 127 - 7, 1), 1, 254)
    codes = (v * np.exp2(127.0 - byte)[:, None, :]).reshape(n, m).astype(np.float32).astype(ml_dtypes.float8_e4m3fn).view(np.uint8)
    words = codes.reshape(n // 512, 128, 4, m).transpose(0, 1, 3, 2)
    return np.ascontiguousarray(words), np.ascontiguousarray(byte.astype(np.uint8).reshape(n // 512, 16, m))


K, T, N, U = 512, 512, 512, 1024


def setup_inputs():
    n = np.random.standard_normal
    s = mx_kscale(K)[:, None]
    packed_xT = pack_weight(n((K, T)) * s)
    return {
        "x_words": packed_xT[0],
        "x_scales": packed_xT[1],
        "mem": n((N, U)).astype(np.float32),
        "w1": (n((K, N)) / np.sqrt(K) / s).astype(np.float32),
        "slot": striped(np.random.permutation(U)[:T]),
    }


def reference(x_words, x_scales, mem, w1, slot):
    xq = unpack_weight(x_words, x_scales)
    y = mxq(f64(w1), 0, "e4m3").T @ xq
    out = f64(mem).copy()
    out[:, unstriped(slot)] = y
    return (out,) + planes(out)

@@ -1,0 +1,131 @@
+from contextlib import ExitStack
+
+import concourse.mybir as mybir
+
+K, T, N, U = 512, 512, 512, 1024
+FLOPS = 2 * K * N * T
+
+F32 = mybir.dt.float32
+BF16 = mybir.dt.bfloat16
+I32 = mybir.dt.int32
+U32 = mybir.dt.uint32
+U16 = mybir.dt.uint16
+U8 = mybir.dt.uint8
+FP8X4 = mybir.dt.float8_e4m3fn_x4
+
+P = 128
+PACK = 4
+LIST = 16
+FIRST = 128
+HALF = N // 2
+CHUNKS = ((0, 512), (512, 768), (768, 1024))
+VECTOR_COLS = 640
+
+
+def tile_picked_wkvput_none_lo_kernel(tc, x_words, x_scales, mem, w1, slot, out_0, out_1, out_2):
+    nc = tc.nc
+    with ExitStack() as ctx:
+        keep = ctx.enter_context(tc.tile_pool(name="keep", bufs=1))
+        psum = ctx.enter_context(tc.psum_pool(name="psum", bufs=1))
+
+        offsets = keep.tile([P, T // LIST], U16, name="offsets")
+        x_sc = keep.tile([P, T], U8, name="x_sc", align_bytes=64)
+        x_first = keep.tile([P, FIRST], I32, name="x_first", align_bytes=64)
+        x_rest = keep.tile([P, T - FIRST], I32, name="x_rest", align_bytes=64)
+        w_raw = [keep.tile([P, PACK, HALF], F32, name="w_raw%d" % h) for h in range(2)]
+        window = [keep.tile([P, U], F32, name="window%d" % t) for t in range(PACK)]
+
+        sc_rows = x_scales[0].bitcast(I32)
+        for q in range(4):
+            src = sc_rows[4 * q : 4 * q + 4, :].unsqueeze(0).broadcast_to([8, 4, T // 4])
+            nc.scalar.dma_start(out=x_sc[32 * q : 32 * q + 32, :].bitcast(I32), in_=src)
+
+        w_rows = w1.rearrange("(p j) c -> p j c", j=PACK)
+        x_cols = x_words[0].rearrange("p c r -> p (c r)").bitcast(I32)
+        mem_rows = mem.rearrange("(p t) c -> p t c", t=PACK)
+        out_rows = out_0.rearrange("(p t) c -> p t c", t=PACK)
+        for h in range(2):
+            nc.sync.dma_start(out=w_raw[h][:], in_=w_rows[:, :, h * HALF : (h + 1) * HALF])
+        nc.sync.dma_start(out=x_first[:], in_=x_cols[:, :FIRST])
+        nc.sync.dma_start(offsets[:], slot)
+        nc.sync.dma_start(out=window[0][:], in_=mem_rows[:, 0, :])
+        nc.sync.dma_start(out=x_rest[:], in_=x_cols[:, FIRST:])
+        for t in range(1, PACK):
+            nc.sync.dma_start(out=window[t][:], in_=mem_rows[:, t, :])
+
+        wg0 = keep.tile([P, P, PACK], BF16, name="wg0", align_bytes=64)
+        wgr = keep.tile([P, 3, P, PACK], BF16, name="wgr", align_bytes=64)
+        mh = P // 2
+        src0 = w_raw[0][:].rearrange("p j (m t) -> p m j t", t=PACK)
+        src1 = w_raw[1][:].rearrange("p j (m t) -> p m j t", t=PACK)
+        wgr_v = wgr[:].rearrange("p t m j -> p m j t")
+        nc.vector.tensor_copy(out=wg0[:, :mh, :], in_=src0[:, :, :, 0])
+        nc.vector.tensor_copy(out=wgr_v[:, :mh, :, :], in_=src0[:, :, :, 1:])
+        nc.vector.tensor_copy(out=wg0[:, mh:, :], in_=src1[:, :, :, 0])
+        nc.scalar.copy(out=wgr_v[:, mh:, :, :], in_=src1[:, :, :, 1:])
+
+        wc0 = keep.tile([P, P], U32, name="wc0", align_bytes=64)
+        ws0 = keep.tile([P, P], U8, name="ws0", align_bytes=64)
+        wcr = keep.tile([P, 3 * P], U32, name="wcr", align_bytes=64)
+        wsr = keep.tile([P, 3 * P], U8, name="wsr", align_bytes=64)
+        nc.vector.quantize_mx(out=wc0[:].bitcast(FP8X4), scales=ws0[:], in_=wg0[:].rearrange("p m j -> p (m j)"))
+
+        def product(out, codes, scales, x_tile, x0, c0, c1):
+            nc.tensor.matmul_mx(out=out, lhsT=codes.bitcast(FP8X4), lhsT_scale=scales,
+                                rhs=x_tile[:, c0 - x0 : c1 - x0].bitcast(FP8X4), rhs_scale=x_sc[:, c0:c1],
+                                start=True, stop=True)
+
+        acc_first = psum.tile([P, FIRST], F32, name="acc_first")
+        y_first = keep.tile([P, FIRST], F32, name="y_first")
+        product(acc_first[:], wc0[:], ws0[:], x_first, 0, 0, FIRST)
+        nc.vector.tensor_copy(out=y_first[:], in_=acc_first[:])
+
+        wgr_flat = wgr[:].rearrange("p t m j -> p (t m j)")
+        nc.vector.quantize_mx(out=wcr[:, :P].bitcast(FP8X4), scales=wsr[:, :P], in_=wgr_flat[:, : PACK * P])
+        nc.vector.quantize_mx(out=wcr[:, P:].bitcast(FP8X4), scales=wsr[:, P:], in_=wgr_flat[:, PACK * P :])
+
+        acc_rest = psum.tile([P, T - FIRST], F32, name="acc_rest")
+        y_rest = keep.tile([P, T - FIRST], F32, name="y_rest")
+        product(acc_rest[:, :128], wc0[:], ws0[:], x_rest, FIRST, 128, 256)
+        product(acc_rest[:, 128:], wc0[:], ws0[:], x_rest, FIRST, 256, 512)
+        nc.scalar.copy(out=y_rest[:], in_=acc_rest[:])
+
+        y = [None]
+        for t in range(1, PACK):
+            acc = psum.tile([P, T], F32, name="acc%d" % t)
+            y_t = keep.tile([P, T], F32, name="y%d" % t)
+            cols = slice((t - 1) * P, t * P)
+            product(acc[:, :128], wcr[:, cols], wsr[:, cols], x_first, 0, 0, 128)
+            product(acc[:, 128:256], wcr[:, cols], wsr[:, cols], x_rest, FIRST, 128, 256)
+            product(acc[:, 256:], wcr[:, cols], wsr[:, cols], x_rest, FIRST, 256, 512)
+            nc.scalar.copy(out=y_t[:], in_=acc[:])
+            y.append(y_t)
+
+        grouped = [keep.tile([P, c1 - c0, PACK], BF16, name="grouped%d" % i, align_bytes=64) for i, (c0, c1) in enumerate(CHUNKS)]
+        for t in range(PACK):
+            if t == 0:
+                nc.vector.tensor_copy(window[0][:].indirect(offsets[:, : FIRST // LIST]), y_first[:])
+                nc.vector.tensor_copy(window[0][:].indirect(offsets[:, FIRST // LIST :]), y_rest[:])
+            else:
+                nc.vector.tensor_copy(window[t][:].indirect(offsets[:]), y[t][:])
+            nc.sync.dma_start(out=out_rows[:, t, :], in_=window[t][:])
+            for i, (c0, c1) in enumerate(CHUNKS):
+                split = min(max(VECTOR_COLS, c0), c1) if t == PACK - 1 else c0
+                if split > c0:
+                    nc.vector.tensor_copy(out=grouped[i][:, : split - c0, t], in_=window[t][:, c0:split])
+                if t == PACK - 2 and c0 < VECTOR_COLS:
+                    src = window[t][:, c0:c1].unsqueeze(2).broadcast_to([P, c1 - c0, 2])
+                    nc.scalar.copy(out=grouped[i][:, :, t:], in_=src)
+                elif split < c1:
+                    nc.scalar.copy(out=grouped[i][:, split - c0 :, t], in_=window[t][:, split:c1])
+
+        o_sc = keep.tile([P, U], U8, name="o_sc", align_bytes=64)
+        o_words = out_1[0].rearrange("p c r -> p (c r)").bitcast(I32)
+        for i, (c0, c1) in enumerate(CHUNKS):
+            codes = keep.tile([P, c1 - c0], I32, name="o_codes%d" % i, align_bytes=64)
+            nc.vector.quantize_mx(out=codes[:].bitcast(FP8X4), scales=o_sc[:, c0:c1], in_=grouped[i][:].rearrange("p c t -> p (c t)"))
+            nc.sync.dma_start(out=o_words[:, c0:c1], in_=codes[:])
+        o_rows = out_2[0].bitcast(I32)
+        for q in range(4):
+            queue = nc.scalar if q % 2 else nc.sync
+            queue.dma_start(out=o_rows[4 * q : 4 * q + 4, :], in_=o_sc[32 * q : 32 * q + 4, :].bitcast(I32))

@@ -8,7 +8,6 @@ FLOPS = 2 * K * N * T
 F32 = mybir.dt.float32
 BF16 = mybir.dt.bfloat16
 I32 = mybir.dt.int32
-U32 = mybir.dt.uint32
 U16 = mybir.dt.uint16
 U8 = mybir.dt.uint8
 FP8X4 = mybir.dt.float8_e4m3fn_x4
@@ -16,10 +15,9 @@ FP8X4 = mybir.dt.float8_e4m3fn_x4
 P = 128
 PACK = 4
 LIST = 16
-FIRST = 128
-HALF = N // 2
-CHUNKS = ((0, 512), (512, 768), (768, 1024))
-VECTOR_COLS = 640
+FIRST = 256
+SPLIT = 512
+PIECES = ((0, 128), (128, 256), (256, 512))
 
 
 def tile_picked_wkvput_none_lo_kernel(tc, x_words, x_scales, mem, w1, slot, out_0, out_1, out_2):
@@ -30,102 +28,97 @@ def tile_picked_wkvput_none_lo_kernel(tc, x_words, x_scales, mem, w1, slot, out_
 
         offsets = keep.tile([P, T // LIST], U16, name="offsets")
         x_sc = keep.tile([P, T], U8, name="x_sc", align_bytes=64)
-        x_first = keep.tile([P, FIRST], I32, name="x_first", align_bytes=64)
-        x_rest = keep.tile([P, T - FIRST], I32, name="x_rest", align_bytes=64)
-        w_raw = [keep.tile([P, PACK, HALF], F32, name="w_raw%d" % h) for h in range(2)]
+        x_half = [keep.tile([P, FIRST], I32, name="x_half%d" % h, align_bytes=64) for h in range(2)]
+        w_raw = [keep.tile([P, 2, N], F32, name="w_raw%d" % h) for h in range(2)]
         window = [keep.tile([P, U], F32, name="window%d" % t) for t in range(PACK)]
 
+        nc.vector.memset(x_sc[:].bitcast(I32), 0)
         sc_rows = x_scales[0].bitcast(I32)
-        for q in range(4):
-            src = sc_rows[4 * q : 4 * q + 4, :].unsqueeze(0).broadcast_to([8, 4, T // 4])
-            nc.scalar.dma_start(out=x_sc[32 * q : 32 * q + 32, :].bitcast(I32), in_=src)
-
         w_rows = w1.rearrange("(p j) c -> p j c", j=PACK)
         x_cols = x_words[0].rearrange("p c r -> p (c r)").bitcast(I32)
         mem_rows = mem.rearrange("(p t) c -> p t c", t=PACK)
         out_rows = out_0.rearrange("(p t) c -> p t c", t=PACK)
-        for h in range(2):
-            nc.sync.dma_start(out=w_raw[h][:], in_=w_rows[:, :, h * HALF : (h + 1) * HALF])
-        nc.sync.dma_start(out=x_first[:], in_=x_cols[:, :FIRST])
-        nc.sync.dma_start(offsets[:], slot)
+        nc.sync.dma_start(out=w_raw[0][:], in_=w_rows[:, :2, :])
+        for q in range(4):
+            nc.sync.dma_start(out=x_sc[32 * q : 32 * q + 4, :].bitcast(I32), in_=sc_rows[4 * q : 4 * q + 4, :])
+        nc.sync.dma_start(out=w_raw[1][:], in_=w_rows[:, 2:, :])
+        nc.sync.dma_start(out=x_half[0][:], in_=x_cols[:, :FIRST])
         nc.sync.dma_start(out=window[0][:], in_=mem_rows[:, 0, :])
-        nc.sync.dma_start(out=x_rest[:], in_=x_cols[:, FIRST:])
+        nc.sync.dma_start(offsets[:], slot)
+        nc.sync.dma_start(out=x_half[1][:], in_=x_cols[:, FIRST:])
         for t in range(1, PACK):
             nc.sync.dma_start(out=window[t][:], in_=mem_rows[:, t, :])
 
-        wg0 = keep.tile([P, P, PACK], BF16, name="wg0", align_bytes=64)
-        wgr = keep.tile([P, 3, P, PACK], BF16, name="wgr", align_bytes=64)
-        mh = P // 2
-        src0 = w_raw[0][:].rearrange("p j (m t) -> p m j t", t=PACK)
-        src1 = w_raw[1][:].rearrange("p j (m t) -> p m j t", t=PACK)
-        wgr_v = wgr[:].rearrange("p t m j -> p m j t")
-        nc.vector.tensor_copy(out=wg0[:, :mh, :], in_=src0[:, :, :, 0])
-        nc.vector.tensor_copy(out=wgr_v[:, :mh, :, :], in_=src0[:, :, :, 1:])
-        nc.vector.tensor_copy(out=wg0[:, mh:, :], in_=src1[:, :, :, 0])
-        nc.scalar.copy(out=wgr_v[:, mh:, :, :], in_=src1[:, :, :, 1:])
+        w_grouped = keep.tile([P, PACK, P, PACK], BF16, name="w_grouped", align_bytes=64)
+        dst = w_grouped[:].rearrange("p t m j -> p m t j")
+        src = [w_raw[h][:].rearrange("p j (m t) -> p m t j", t=PACK) for h in range(2)]
+        nc.vector.tensor_copy(out=dst[:, :, :, :2], in_=src[0])
+        nc.vector.tensor_copy(out=dst[:, :, 0, 2:], in_=src[1][:, :, 0, :])
+        nc.vector.tensor_copy(out=dst[:, :, 1, 2:], in_=src[1][:, :, 1, :])
+        nc.scalar.copy(out=dst[:, :, 2:, 2:], in_=src[1][:, :, 2:, :])
 
-        wc0 = keep.tile([P, P], U32, name="wc0", align_bytes=64)
-        ws0 = keep.tile([P, P], U8, name="ws0", align_bytes=64)
-        wcr = keep.tile([P, 3 * P], U32, name="wcr", align_bytes=64)
-        wsr = keep.tile([P, 3 * P], U8, name="wsr", align_bytes=64)
-        nc.vector.quantize_mx(out=wc0[:].bitcast(FP8X4), scales=ws0[:], in_=wg0[:].rearrange("p m j -> p (m j)"))
+        w_codes = keep.tile([P, N], I32, name="w_codes", align_bytes=64)
+        w_sc = keep.tile([P, N], U8, name="w_sc", align_bytes=64)
+        w_flat = w_grouped[:].rearrange("p t m j -> p (t m j)")
+        for c0, c1 in ((0, 128), (128, 256), (256, 512)):
+            nc.vector.quantize_mx(out=w_codes[:, c0:c1].bitcast(FP8X4), scales=w_sc[:, c0:c1], in_=w_flat[:, PACK * c0 : PACK * c1])
 
-        def product(out, codes, scales, x_tile, x0, c0, c1):
-            nc.tensor.matmul_mx(out=out, lhsT=codes.bitcast(FP8X4), lhsT_scale=scales,
-                                rhs=x_tile[:, c0 - x0 : c1 - x0].bitcast(FP8X4), rhs_scale=x_sc[:, c0:c1],
+        def product(out, t, c0, c1):
+            rows = slice(t * P, (t + 1) * P)
+            h = c0 // FIRST
+            nc.tensor.matmul_mx(out=out, lhsT=w_codes[:, rows].bitcast(FP8X4), lhsT_scale=w_sc[:, rows],
+                                rhs=x_half[h][:, c0 - h * FIRST : c1 - h * FIRST].bitcast(FP8X4), rhs_scale=x_sc[:, c0:c1],
                                 start=True, stop=True)
 
-        acc_first = psum.tile([P, FIRST], F32, name="acc_first")
-        y_first = keep.tile([P, FIRST], F32, name="y_first")
-        product(acc_first[:], wc0[:], ws0[:], x_first, 0, 0, FIRST)
-        nc.vector.tensor_copy(out=y_first[:], in_=acc_first[:])
-
-        wgr_flat = wgr[:].rearrange("p t m j -> p (t m j)")
-        nc.vector.quantize_mx(out=wcr[:, :P].bitcast(FP8X4), scales=wsr[:, :P], in_=wgr_flat[:, : PACK * P])
-        nc.vector.quantize_mx(out=wcr[:, P:].bitcast(FP8X4), scales=wsr[:, P:], in_=wgr_flat[:, PACK * P :])
-
-        acc_rest = psum.tile([P, T - FIRST], F32, name="acc_rest")
-        y_rest = keep.tile([P, T - FIRST], F32, name="y_rest")
-        product(acc_rest[:, :128], wc0[:], ws0[:], x_rest, FIRST, 128, 256)
-        product(acc_rest[:, 128:], wc0[:], ws0[:], x_rest, FIRST, 256, 512)
-        nc.scalar.copy(out=y_rest[:], in_=acc_rest[:])
-
+        y0 = []
+        for c0, c1 in PIECES:
+            acc = psum.tile([P, c1 - c0], F32, name="acc0_%d" % c0)
+            y_h = keep.tile([P, c1 - c0], F32, name="y0_%d" % c0)
+            product(acc[:], 0, c0, c1)
+            nc.scalar.copy(out=y_h[:], in_=acc[:])
+            y0.append(y_h)
         y = [None]
         for t in range(1, PACK):
             acc = psum.tile([P, T], F32, name="acc%d" % t)
             y_t = keep.tile([P, T], F32, name="y%d" % t)
-            cols = slice((t - 1) * P, t * P)
-            product(acc[:, :128], wcr[:, cols], wsr[:, cols], x_first, 0, 0, 128)
-            product(acc[:, 128:256], wcr[:, cols], wsr[:, cols], x_rest, FIRST, 128, 256)
-            product(acc[:, 256:], wcr[:, cols], wsr[:, cols], x_rest, FIRST, 256, 512)
+            for h in range(2):
+                product(acc[:, h * FIRST : (h + 1) * FIRST], t, h * FIRST, (h + 1) * FIRST)
             nc.scalar.copy(out=y_t[:], in_=acc[:])
             y.append(y_t)
 
-        grouped = [keep.tile([P, c1 - c0, PACK], BF16, name="grouped%d" % i, align_bytes=64) for i, (c0, c1) in enumerate(CHUNKS)]
+        left = keep.tile([P, SPLIT, PACK], BF16, name="left", align_bytes=64)
+        right = keep.tile([P, U - SPLIT, PACK], BF16, name="right", align_bytes=64)
         for t in range(PACK):
             if t == 0:
-                nc.vector.tensor_copy(window[0][:].indirect(offsets[:, : FIRST // LIST]), y_first[:])
-                nc.vector.tensor_copy(window[0][:].indirect(offsets[:, FIRST // LIST :]), y_rest[:])
+                for h, (c0, c1) in enumerate(PIECES):
+                    nc.vector.tensor_copy(window[0][:].indirect(offsets[:, c0 // LIST : c1 // LIST]), y0[h][:])
             else:
                 nc.vector.tensor_copy(window[t][:].indirect(offsets[:]), y[t][:])
             nc.sync.dma_start(out=out_rows[:, t, :], in_=window[t][:])
-            for i, (c0, c1) in enumerate(CHUNKS):
-                split = min(max(VECTOR_COLS, c0), c1) if t == PACK - 1 else c0
-                if split > c0:
-                    nc.vector.tensor_copy(out=grouped[i][:, : split - c0, t], in_=window[t][:, c0:split])
-                if t == PACK - 2 and c0 < VECTOR_COLS:
-                    src = window[t][:, c0:c1].unsqueeze(2).broadcast_to([P, c1 - c0, 2])
-                    nc.scalar.copy(out=grouped[i][:, :, t:], in_=src)
-                elif split < c1:
-                    nc.scalar.copy(out=grouped[i][:, split - c0 :, t], in_=window[t][:, split:c1])
+            if t < 2:
+                nc.scalar.copy(out=left[:, :, t], in_=window[t][:, :SPLIT])
+            elif t == 2:
+                nc.scalar.copy(out=left[:, :, t:], in_=window[t][:, :SPLIT].unsqueeze(2).broadcast_to([P, SPLIT, 2]))
+            else:
+                nc.vector.tensor_copy(out=left[:, :256, t], in_=window[t][:, :256])
+                nc.vector.tensor_copy(out=left[:, 256:, t], in_=window[t][:, 256:SPLIT])
+            if t < 3:
+                nc.scalar.copy(out=right[:, :, t], in_=window[t][:, SPLIT:])
+            else:
+                for c0, c1 in ((0, 256), (256, 384), (384, 512)):
+                    nc.scalar.copy(out=right[:, c0:c1, t], in_=window[t][:, SPLIT + c0 : SPLIT + c1])
 
         o_sc = keep.tile([P, U], U8, name="o_sc", align_bytes=64)
+        o_codes = keep.tile([P, U], I32, name="o_codes", align_bytes=64)
         o_words = out_1[0].rearrange("p c r -> p (c r)").bitcast(I32)
-        for i, (c0, c1) in enumerate(CHUNKS):
-            codes = keep.tile([P, c1 - c0], I32, name="o_codes%d" % i, align_bytes=64)
-            nc.vector.quantize_mx(out=codes[:].bitcast(FP8X4), scales=o_sc[:, c0:c1], in_=grouped[i][:].rearrange("p c t -> p (c t)"))
-            nc.sync.dma_start(out=o_words[:, c0:c1], in_=codes[:])
+        stored = 0
+        for c0, c1 in ((0, 256), (256, 512), (512, 768), (768, 896), (896, 1024)):
+            part = left[:, c0:c1, :] if c0 < SPLIT else right[:, c0 - SPLIT : c1 - SPLIT, :]
+            nc.vector.quantize_mx(out=o_codes[:, c0:c1].bitcast(FP8X4), scales=o_sc[:, c0:c1], in_=part.rearrange("p c t -> p (c t)"))
+            if c1 in (512, 768, 1024):
+                nc.sync.dma_start(out=o_words[:, stored:c1], in_=o_codes[:, stored:c1])
+                stored = c1
         o_rows = out_2[0].bitcast(I32)
         for q in range(4):
-            queue = nc.scalar if q % 2 else nc.sync
+            queue = nc.sync if q == 3 else nc.scalar
             queue.dma_start(out=o_rows[4 * q : 4 * q + 4, :], in_=o_sc[32 * q : 32 * q + 4, :].bitcast(I32))

@@ -16,8 +16,8 @@ P = 128
 PACK = 4
 LIST = 16
 FIRST = 256
-SPLIT = 512
-PIECES = ((0, 128), (128, 256), (256, 512))
+SPLIT = 576
+PIECES = ((0, 256), (256, 512))
 
 
 def tile_picked_wkvput_none_lo_kernel(tc, x_words, x_scales, mem, w1, slot, out_0, out_1, out_2):
@@ -49,19 +49,29 @@ def tile_picked_wkvput_none_lo_kernel(tc, x_words, x_scales, mem, w1, slot, out_
         for t in range(1, PACK):
             nc.sync.dma_start(out=window[t][:], in_=mem_rows[:, t, :])
 
-        w_grouped = keep.tile([P, PACK, P, PACK], BF16, name="w_grouped", align_bytes=64)
-        dst = w_grouped[:].rearrange("p t m j -> p m t j")
-        src = [w_raw[h][:].rearrange("p j (m t) -> p m t j", t=PACK) for h in range(2)]
-        nc.vector.tensor_copy(out=dst[:, :, :, :2], in_=src[0])
-        nc.vector.tensor_copy(out=dst[:, :, 0, 2:], in_=src[1][:, :, 0, :])
-        nc.vector.tensor_copy(out=dst[:, :, 1, 2:], in_=src[1][:, :, 1, :])
-        nc.scalar.copy(out=dst[:, :, 2:, 2:], in_=src[1][:, :, 2:, :])
-
         w_codes = keep.tile([P, N], I32, name="w_codes", align_bytes=64)
         w_sc = keep.tile([P, N], U8, name="w_sc", align_bytes=64)
-        w_flat = w_grouped[:].rearrange("p t m j -> p (t m j)")
-        for c0, c1 in ((0, 128), (128, 256), (256, 512)):
-            nc.vector.quantize_mx(out=w_codes[:, c0:c1].bitcast(FP8X4), scales=w_sc[:, c0:c1], in_=w_flat[:, PACK * c0 : PACK * c1])
+        src = [w_raw[h][:].rearrange("p j (m t) -> p m t j", t=PACK) for h in range(2)]
+
+        def quantize_w(t, grouped):
+            rows = slice(t * P, (t + 1) * P)
+            nc.vector.quantize_mx(out=w_codes[:, rows].bitcast(FP8X4), scales=w_sc[:, rows], in_=grouped.rearrange("p m j -> p (m j)"))
+
+        g0 = keep.tile([P, P, PACK], BF16, name="g0", tag="outer", align_bytes=64)
+        g1 = keep.tile([P, P, PACK], BF16, name="g1", align_bytes=64)
+        g2 = keep.tile([P, P, PACK], BF16, name="g2", align_bytes=64)
+        for h in range(2):
+            pair = slice(2 * h, 2 * h + 2)
+            nc.vector.tensor_copy(out=g0[:, :, pair], in_=src[h][:, :, 0, :])
+            nc.vector.tensor_copy(out=g1[:, :, pair], in_=src[h][:, :, 1, :])
+            nc.scalar.copy(out=g2[:, :, pair], in_=src[h][:, :, 2, :])
+        quantize_w(0, g0[:])
+        g3 = keep.tile([P, P, PACK], BF16, name="g3", tag="outer", align_bytes=64)
+        for h in range(2):
+            nc.vector.tensor_copy(out=g3[:, :, 2 * h : 2 * h + 2], in_=src[h][:, :, 3, :])
+        quantize_w(1, g1[:])
+        quantize_w(2, g2[:])
+        quantize_w(3, g3[:])
 
         def product(out, t, c0, c1):
             rows = slice(t * P, (t + 1) * P)
@@ -105,17 +115,17 @@ def tile_picked_wkvput_none_lo_kernel(tc, x_words, x_scales, mem, w1, slot, out_
             if t < 3:
                 nc.scalar.copy(out=right[:, :, t], in_=window[t][:, SPLIT:])
             else:
-                for c0, c1 in ((0, 256), (256, 384), (384, 512)):
+                for c0, c1 in ((0, 256), (256, 384), (384, 448)):
                     nc.scalar.copy(out=right[:, c0:c1, t], in_=window[t][:, SPLIT + c0 : SPLIT + c1])
 
         o_sc = keep.tile([P, U], U8, name="o_sc", align_bytes=64)
         o_codes = keep.tile([P, U], I32, name="o_codes", align_bytes=64)
         o_words = out_1[0].rearrange("p c r -> p (c r)").bitcast(I32)
         stored = 0
-        for c0, c1 in ((0, 256), (256, 512), (512, 768), (768, 896), (896, 1024)):
+        for c0, c1 in ((0, 256), (256, 512), (512, 576), (576, 832), (832, 960), (960, 1024)):
             part = left[:, c0:c1, :] if c0 < SPLIT else right[:, c0 - SPLIT : c1 - SPLIT, :]
             nc.vector.quantize_mx(out=o_codes[:, c0:c1].bitcast(FP8X4), scales=o_sc[:, c0:c1], in_=part.rearrange("p c t -> p (c t)"))
-            if c1 in (512, 768, 1024):
+            if c1 in (512, 832, 1024):
                 nc.sync.dma_start(out=o_words[:, stored:c1], in_=o_codes[:, stored:c1])
                 stored = c1
         o_rows = out_2[0].bitcast(I32)

@@ -16,8 +16,10 @@ P = 128
 PACK = 4
 LIST = 16
 FIRST = 256
-SPLIT = 576
-PIECES = ((0, 256), (256, 512))
+SPLIT = 512
+PIECE = 256
+X_LOADS = ((0, FIRST), (FIRST, T))
+PASSES = X_LOADS
 
 
 def tile_picked_wkvput_none_lo_kernel(tc, x_words, x_scales, mem, w1, slot, out_0, out_1, out_2):
@@ -28,7 +30,7 @@ def tile_picked_wkvput_none_lo_kernel(tc, x_words, x_scales, mem, w1, slot, out_
 
         offsets = keep.tile([P, T // LIST], U16, name="offsets")
         x_sc = keep.tile([P, T], U8, name="x_sc", align_bytes=64)
-        x_half = [keep.tile([P, FIRST], I32, name="x_half%d" % h, align_bytes=64) for h in range(2)]
+        x_part = [keep.tile([P, c1 - c0], I32, name="x_part%d" % c0, align_bytes=64) for c0, c1 in X_LOADS]
         w_raw = [keep.tile([P, 2, N], F32, name="w_raw%d" % h) for h in range(2)]
         window = [keep.tile([P, U], F32, name="window%d" % t) for t in range(PACK)]
 
@@ -39,60 +41,62 @@ def tile_picked_wkvput_none_lo_kernel(tc, x_words, x_scales, mem, w1, slot, out_
         mem_rows = mem.rearrange("(p t) c -> p t c", t=PACK)
         out_rows = out_0.rearrange("(p t) c -> p t c", t=PACK)
         nc.sync.dma_start(out=w_raw[0][:], in_=w_rows[:, :2, :])
-        for q in range(4):
-            nc.sync.dma_start(out=x_sc[32 * q : 32 * q + 4, :].bitcast(I32), in_=sc_rows[4 * q : 4 * q + 4, :])
+        for r in range(4):
+            nc.sync.dma_start(out=x_sc[r:P:32, :].bitcast(I32), in_=sc_rows[r:16:4, :])
         nc.sync.dma_start(out=w_raw[1][:], in_=w_rows[:, 2:, :])
-        nc.sync.dma_start(out=x_half[0][:], in_=x_cols[:, :FIRST])
+        nc.sync.dma_start(out=x_part[0][:], in_=x_cols[:, :FIRST])
         nc.sync.dma_start(out=window[0][:], in_=mem_rows[:, 0, :])
         nc.sync.dma_start(offsets[:], slot)
-        nc.sync.dma_start(out=x_half[1][:], in_=x_cols[:, FIRST:])
+        nc.sync.dma_start(out=x_part[1][:], in_=x_cols[:, FIRST:])
         for t in range(1, PACK):
             nc.sync.dma_start(out=window[t][:], in_=mem_rows[:, t, :])
 
         w_codes = keep.tile([P, N], I32, name="w_codes", align_bytes=64)
         w_sc = keep.tile([P, N], U8, name="w_sc", align_bytes=64)
         src = [w_raw[h][:].rearrange("p j (m t) -> p m t j", t=PACK) for h in range(2)]
+        grouped = [keep.tile([P, P, PACK], BF16, name="grouped%d" % t, tag="grouped%d" % t, align_bytes=64) for t in range(PACK - 1)]
 
-        def quantize_w(t, grouped):
+        def deal(copy, t, h):
+            copy(out=grouped[t][:, :, 2 * h : 2 * h + 2], in_=src[h][:, :, t, :])
+
+        def quantize_w(t):
             rows = slice(t * P, (t + 1) * P)
-            nc.vector.quantize_mx(out=w_codes[:, rows].bitcast(FP8X4), scales=w_sc[:, rows], in_=grouped.rearrange("p m j -> p (m j)"))
+            nc.vector.quantize_mx(out=w_codes[:, rows].bitcast(FP8X4), scales=w_sc[:, rows], in_=grouped[t][:].rearrange("p m j -> p (m j)"))
 
-        g0 = keep.tile([P, P, PACK], BF16, name="g0", tag="outer", align_bytes=64)
-        g1 = keep.tile([P, P, PACK], BF16, name="g1", align_bytes=64)
-        g2 = keep.tile([P, P, PACK], BF16, name="g2", align_bytes=64)
         for h in range(2):
-            pair = slice(2 * h, 2 * h + 2)
-            nc.vector.tensor_copy(out=g0[:, :, pair], in_=src[h][:, :, 0, :])
-            nc.vector.tensor_copy(out=g1[:, :, pair], in_=src[h][:, :, 1, :])
-            nc.scalar.copy(out=g2[:, :, pair], in_=src[h][:, :, 2, :])
-        quantize_w(0, g0[:])
-        g3 = keep.tile([P, P, PACK], BF16, name="g3", tag="outer", align_bytes=64)
+            deal(nc.vector.tensor_copy, 0, h)
+            deal(nc.vector.tensor_copy, 1, h)
+            deal(nc.scalar.copy, 2, h)
+        quantize_w(0)
+        grouped.append(keep.tile([P, P, PACK], BF16, name="grouped3", tag="grouped0", align_bytes=64))
         for h in range(2):
-            nc.vector.tensor_copy(out=g3[:, :, 2 * h : 2 * h + 2], in_=src[h][:, :, 3, :])
-        quantize_w(1, g1[:])
-        quantize_w(2, g2[:])
-        quantize_w(3, g3[:])
+            deal(nc.vector.tensor_copy, 3, h)
+        for t in range(1, PACK):
+            quantize_w(t)
 
         def product(out, t, c0, c1):
             rows = slice(t * P, (t + 1) * P)
-            h = c0 // FIRST
+            h = 0 if c0 < FIRST else 1
+            base = X_LOADS[h][0]
             nc.tensor.matmul_mx(out=out, lhsT=w_codes[:, rows].bitcast(FP8X4), lhsT_scale=w_sc[:, rows],
-                                rhs=x_half[h][:, c0 - h * FIRST : c1 - h * FIRST].bitcast(FP8X4), rhs_scale=x_sc[:, c0:c1],
+                                rhs=x_part[h][:, c0 - base : c1 - base].bitcast(FP8X4), rhs_scale=x_sc[:, c0:c1],
                                 start=True, stop=True)
 
         y0 = []
-        for c0, c1 in PIECES:
+        for c0, c1 in X_LOADS:
             acc = psum.tile([P, c1 - c0], F32, name="acc0_%d" % c0)
             y_h = keep.tile([P, c1 - c0], F32, name="y0_%d" % c0)
-            product(acc[:], 0, c0, c1)
+            for d0, d1 in PASSES:
+                if c0 <= d0 < c1:
+                    product(acc[:, d0 - c0 : d1 - c0], 0, d0, d1)
             nc.scalar.copy(out=y_h[:], in_=acc[:])
             y0.append(y_h)
         y = [None]
         for t in range(1, PACK):
             acc = psum.tile([P, T], F32, name="acc%d" % t)
             y_t = keep.tile([P, T], F32, name="y%d" % t)
-            for h in range(2):
-                product(acc[:, h * FIRST : (h + 1) * FIRST], t, h * FIRST, (h + 1) * FIRST)
+            for d0, d1 in PASSES:
+                product(acc[:, d0:d1], t, d0, d1)
             nc.scalar.copy(out=y_t[:], in_=acc[:])
             y.append(y_t)
 
@@ -100,7 +104,7 @@ def tile_picked_wkvput_none_lo_kernel(tc, x_words, x_scales, mem, w1, slot, out_
         right = keep.tile([P, U - SPLIT, PACK], BF16, name="right", align_bytes=64)
         for t in range(PACK):
             if t == 0:
-                for h, (c0, c1) in enumerate(PIECES):
+                for h, (c0, c1) in enumerate(X_LOADS):
                     nc.vector.tensor_copy(window[0][:].indirect(offsets[:, c0 // LIST : c1 // LIST]), y0[h][:])
             else:
                 nc.vector.tensor_copy(window[t][:].indirect(offsets[:]), y[t][:])
@@ -110,25 +114,25 @@ def tile_picked_wkvput_none_lo_kernel(tc, x_words, x_scales, mem, w1, slot, out_
             elif t == 2:
                 nc.scalar.copy(out=left[:, :, t:], in_=window[t][:, :SPLIT].unsqueeze(2).broadcast_to([P, SPLIT, 2]))
             else:
-                nc.vector.tensor_copy(out=left[:, :256, t], in_=window[t][:, :256])
-                nc.vector.tensor_copy(out=left[:, 256:, t], in_=window[t][:, 256:SPLIT])
+                for c0 in range(0, SPLIT, PIECE):
+                    nc.vector.tensor_copy(out=left[:, c0 : c0 + PIECE, t], in_=window[t][:, c0 : c0 + PIECE])
             if t < 3:
                 nc.scalar.copy(out=right[:, :, t], in_=window[t][:, SPLIT:])
             else:
-                for c0, c1 in ((0, 256), (256, 384), (384, 448)):
-                    nc.scalar.copy(out=right[:, c0:c1, t], in_=window[t][:, SPLIT + c0 : SPLIT + c1])
+                for c0 in range(0, U - SPLIT, PIECE):
+                    nc.scalar.copy(out=right[:, c0 : c0 + PIECE, t], in_=window[t][:, SPLIT + c0 : SPLIT + c0 + PIECE])
 
         o_sc = keep.tile([P, U], U8, name="o_sc", align_bytes=64)
         o_codes = keep.tile([P, U], I32, name="o_codes", align_bytes=64)
         o_words = out_1[0].rearrange("p c r -> p (c r)").bitcast(I32)
         stored = 0
-        for c0, c1 in ((0, 256), (256, 512), (512, 576), (576, 832), (832, 960), (960, 1024)):
+        for c0, c1 in ((0, 256), (256, 384), (384, 512), (512, 768), (768, 1024)):
             part = left[:, c0:c1, :] if c0 < SPLIT else right[:, c0 - SPLIT : c1 - SPLIT, :]
             nc.vector.quantize_mx(out=o_codes[:, c0:c1].bitcast(FP8X4), scales=o_sc[:, c0:c1], in_=part.rearrange("p c t -> p (c t)"))
-            if c1 in (512, 832, 1024):
+            if c1 in (384, 768, 1024):
                 nc.sync.dma_start(out=o_words[:, stored:c1], in_=o_codes[:, stored:c1])
                 stored = c1
         o_rows = out_2[0].bitcast(I32)
-        for q in range(4):
-            queue = nc.sync if q == 3 else nc.scalar
-            queue.dma_start(out=o_rows[4 * q : 4 * q + 4, :], in_=o_sc[32 * q : 32 * q + 4, :].bitcast(I32))
+        for r in range(4):
+            queue = nc.sync if r < 2 else nc.scalar
+            queue.dma_start(out=o_rows[r:16:4, :], in_=o_sc[r:P:32, :].bitcast(I32))

@@ -17,9 +17,9 @@ PACK = 4
 LIST = 16
 FIRST = 256
 SPLIT = 512
+BETWEEN = 192
 PIECE = 256
 X_LOADS = ((0, FIRST), (FIRST, T))
-PASSES = X_LOADS
 
 
 def tile_picked_wkvput_none_lo_kernel(tc, x_words, x_scales, mem, w1, slot, out_0, out_1, out_2):
@@ -42,13 +42,15 @@ def tile_picked_wkvput_none_lo_kernel(tc, x_words, x_scales, mem, w1, slot, out_
         out_rows = out_0.rearrange("(p t) c -> p t c", t=PACK)
         nc.sync.dma_start(out=w_raw[0][:], in_=w_rows[:, :2, :])
         for r in range(4):
-            nc.sync.dma_start(out=x_sc[r:P:32, :].bitcast(I32), in_=sc_rows[r:16:4, :])
+            queue = nc.sync if r % 2 else nc.scalar
+            queue.dma_start(out=x_sc[r:P:32, :].bitcast(I32), in_=sc_rows[r:16:4, :])
         nc.sync.dma_start(out=w_raw[1][:], in_=w_rows[:, 2:, :])
         nc.sync.dma_start(out=x_part[0][:], in_=x_cols[:, :FIRST])
         nc.sync.dma_start(out=window[0][:], in_=mem_rows[:, 0, :])
         nc.sync.dma_start(offsets[:], slot)
+        nc.sync.dma_start(out=window[1][:], in_=mem_rows[:, 1, :])
         nc.sync.dma_start(out=x_part[1][:], in_=x_cols[:, FIRST:])
-        for t in range(1, PACK):
+        for t in range(2, PACK):
             nc.sync.dma_start(out=window[t][:], in_=mem_rows[:, t, :])
 
         w_codes = keep.tile([P, N], I32, name="w_codes", align_bytes=64)
@@ -82,32 +84,27 @@ def tile_picked_wkvput_none_lo_kernel(tc, x_words, x_scales, mem, w1, slot, out_
                                 rhs=x_part[h][:, c0 - base : c1 - base].bitcast(FP8X4), rhs_scale=x_sc[:, c0:c1],
                                 start=True, stop=True)
 
-        y0 = []
+        y = [keep.tile([P, T], F32, name="y%d" % t) for t in range(PACK)]
         for c0, c1 in X_LOADS:
-            acc = psum.tile([P, c1 - c0], F32, name="acc0_%d" % c0)
-            y_h = keep.tile([P, c1 - c0], F32, name="y0_%d" % c0)
-            for d0, d1 in PASSES:
-                if c0 <= d0 < c1:
-                    product(acc[:, d0 - c0 : d1 - c0], 0, d0, d1)
-            nc.scalar.copy(out=y_h[:], in_=acc[:])
-            y0.append(y_h)
-        y = [None]
-        for t in range(1, PACK):
+            for t in range(2):
+                acc = psum.tile([P, c1 - c0], F32, name="acc%d_%d" % (t, c0))
+                product(acc[:], t, c0, c1)
+                nc.scalar.copy(out=y[t][:, c0:c1], in_=acc[:])
+        for t in range(2, PACK):
             acc = psum.tile([P, T], F32, name="acc%d" % t)
-            y_t = keep.tile([P, T], F32, name="y%d" % t)
-            for d0, d1 in PASSES:
-                product(acc[:, d0:d1], t, d0, d1)
-            nc.scalar.copy(out=y_t[:], in_=acc[:])
-            y.append(y_t)
+            for c0, c1 in X_LOADS:
+                product(acc[:, c0:c1], t, c0, c1)
+            nc.scalar.copy(out=y[t][:], in_=acc[:])
+
+        def scatter(t, c0, c1):
+            nc.vector.tensor_copy(window[t][:].indirect(offsets[:, c0 // LIST : c1 // LIST]), y[t][:, c0:c1])
 
         left = keep.tile([P, SPLIT, PACK], BF16, name="left", align_bytes=64)
         right = keep.tile([P, U - SPLIT, PACK], BF16, name="right", align_bytes=64)
+        scatter(0, 0, FIRST)
+        scatter(1, 0, BETWEEN)
         for t in range(PACK):
-            if t == 0:
-                for h, (c0, c1) in enumerate(X_LOADS):
-                    nc.vector.tensor_copy(window[0][:].indirect(offsets[:, c0 // LIST : c1 // LIST]), y0[h][:])
-            else:
-                nc.vector.tensor_copy(window[t][:].indirect(offsets[:]), y[t][:])
+            scatter(t, (FIRST, BETWEEN, 0, 0)[t], T)
             nc.sync.dma_start(out=out_rows[:, t, :], in_=window[t][:])
             if t < 2:
                 nc.scalar.copy(out=left[:, :, t], in_=window[t][:, :SPLIT])
@@ -116,17 +113,20 @@ def tile_picked_wkvput_none_lo_kernel(tc, x_words, x_scales, mem, w1, slot, out_
             else:
                 for c0 in range(0, SPLIT, PIECE):
                     nc.vector.tensor_copy(out=left[:, c0 : c0 + PIECE, t], in_=window[t][:, c0 : c0 + PIECE])
-            if t < 3:
+            if t == 0:
+                nc.gpsimd.tensor_scalar(out=right[:, :, :2], in0=window[0][:, SPLIT:].unsqueeze(2).broadcast_to([P, U - SPLIT, 2]),
+                                        scalar1=1.0, scalar2=-0.0, op0=mybir.AluOpType.mult, op1=mybir.AluOpType.add)
+            elif t < 3:
                 nc.scalar.copy(out=right[:, :, t], in_=window[t][:, SPLIT:])
             else:
-                for c0 in range(0, U - SPLIT, PIECE):
-                    nc.scalar.copy(out=right[:, c0 : c0 + PIECE, t], in_=window[t][:, SPLIT + c0 : SPLIT + c0 + PIECE])
+                for c0, c1 in ((0, 256), (256, 384), (384, 512)):
+                    nc.scalar.copy(out=right[:, c0:c1, t], in_=window[t][:, SPLIT + c0 : SPLIT + c1])
 
         o_sc = keep.tile([P, U], U8, name="o_sc", align_bytes=64)
         o_codes = keep.tile([P, U], I32, name="o_codes", align_bytes=64)
         o_words = out_1[0].rearrange("p c r -> p (c r)").bitcast(I32)
         stored = 0
-        for c0, c1 in ((0, 256), (256, 384), (384, 512), (512, 768), (768, 1024)):
+        for c0, c1 in ((0, 256), (256, 384), (384, 512), (512, 768), (768, 896), (896, 1024)):
             part = left[:, c0:c1, :] if c0 < SPLIT else right[:, c0 - SPLIT : c1 - SPLIT, :]
             nc.vector.quantize_mx(out=o_codes[:, c0:c1].bitcast(FP8X4), scales=o_sc[:, c0:c1], in_=part.rearrange("p c t -> p (c t)"))
             if c1 in (384, 768, 1024):

@@ -109,7 +109,8 @@ def tile_picked_wkvput_none_lo_kernel(tc, x_words, x_scales, mem, w1, slot, out_
             if t < 2:
                 nc.scalar.copy(out=left[:, :, t], in_=window[t][:, :SPLIT])
             elif t == 2:
-                nc.scalar.copy(out=left[:, :, t:], in_=window[t][:, :SPLIT].unsqueeze(2).broadcast_to([P, SPLIT, 2]))
+                nc.gpsimd.tensor_scalar(out=left[:, :, t:], in0=window[t][:, :SPLIT].unsqueeze(2).broadcast_to([P, SPLIT, 2]),
+                                        scalar1=1.0, scalar2=-0.0, op0=mybir.AluOpType.mult, op1=mybir.AluOpType.add)
             else:
                 for c0 in range(0, SPLIT, PIECE):
                     nc.vector.tensor_copy(out=left[:, c0 : c0 + PIECE, t], in_=window[t][:, c0 : c0 + PIECE])

@@ -41,10 +41,10 @@ def tile_picked_wkvput_none_lo_kernel(tc, x_words, x_scales, mem, w1, slot, out_
         mem_rows = mem.rearrange("(p t) c -> p t c", t=PACK)
         out_rows = out_0.rearrange("(p t) c -> p t c", t=PACK)
         nc.sync.dma_start(out=w_raw[0][:], in_=w_rows[:, :2, :])
+        nc.sync.dma_start(out=w_raw[1][:], in_=w_rows[:, 2:, :])
         for r in range(4):
             queue = nc.sync if r % 2 else nc.scalar
             queue.dma_start(out=x_sc[r:P:32, :].bitcast(I32), in_=sc_rows[r:16:4, :])
-        nc.sync.dma_start(out=w_raw[1][:], in_=w_rows[:, 2:, :])
         nc.sync.dma_start(out=x_part[0][:], in_=x_cols[:, :FIRST])
         nc.sync.dma_start(out=window[0][:], in_=mem_rows[:, 0, :])
         nc.sync.dma_start(offsets[:], slot)
@@ -56,7 +56,7 @@ def tile_picked_wkvput_none_lo_kernel(tc, x_words, x_scales, mem, w1, slot, out_
         w_codes = keep.tile([P, N], I32, name="w_codes", align_bytes=64)
         w_sc = keep.tile([P, N], U8, name="w_sc", align_bytes=64)
         src = [w_raw[h][:].rearrange("p j (m t) -> p m t j", t=PACK) for h in range(2)]
-        grouped = [keep.tile([P, P, PACK], BF16, name="grouped%d" % t, tag="grouped%d" % t, align_bytes=64) for t in range(PACK - 1)]
+        grouped = [keep.tile([P, P, PACK], BF16, name="grouped%d" % t, align_bytes=64) for t in range(PACK)]
 
         def deal(copy, t, h):
             copy(out=grouped[t][:, :, 2 * h : 2 * h + 2], in_=src[h][:, :, t, :])
@@ -69,11 +69,8 @@ def tile_picked_wkvput_none_lo_kernel(tc, x_words, x_scales, mem, w1, slot, out_
             deal(nc.vector.tensor_copy, 0, h)
             deal(nc.vector.tensor_copy, 1, h)
             deal(nc.scalar.copy, 2, h)
-        quantize_w(0)
-        grouped.append(keep.tile([P, P, PACK], BF16, name="grouped3", tag="grouped0", align_bytes=64))
-        for h in range(2):
-            deal(nc.vector.tensor_copy, 3, h)
-        for t in range(1, PACK):
+            deal(nc.scalar.copy, 3, h)
+        for t in range(PACK):
             quantize_w(t)
 
         def product(out, t, c0, c1):
@@ -87,9 +84,11 @@ def tile_picked_wkvput_none_lo_kernel(tc, x_words, x_scales, mem, w1, slot, out_
         y = [keep.tile([P, T], F32, name="y%d" % t) for t in range(PACK)]
         for c0, c1 in X_LOADS:
             for t in range(2):
-                acc = psum.tile([P, c1 - c0], F32, name="acc%d_%d" % (t, c0))
-                product(acc[:], t, c0, c1)
-                nc.scalar.copy(out=y[t][:, c0:c1], in_=acc[:])
+                step = P if (t, c0) == (0, 0) else c1 - c0
+                for d0 in range(c0, c1, step):
+                    acc = psum.tile([P, step], F32, name="acc%d_%d" % (t, d0))
+                    product(acc[:], t, d0, d0 + step)
+                    nc.scalar.copy(out=y[t][:, d0 : d0 + step], in_=acc[:])
         for t in range(2, PACK):
             acc = psum.tile([P, T], F32, name="acc%d" % t)
             for c0, c1 in X_LOADS:
@@ -115,7 +114,7 @@ def tile_picked_wkvput_none_lo_kernel(tc, x_words, x_scales, mem, w1, slot, out_
                 for c0 in range(0, SPLIT, PIECE):
                     nc.vector.tensor_copy(out=left[:, c0 : c0 + PIECE, t], in_=window[t][:, c0 : c0 + PIECE])
             if t == 0:
-                nc.gpsimd.tensor_scalar(out=right[:, :, :2], in0=window[0][:, SPLIT:].unsqueeze(2).broadcast_to([P, U - SPLIT, 2]),
+                nc.gpsimd.tensor_scalar(out=right[:, :, t : t + 2], in0=window[t][:, SPLIT:].unsqueeze(2).broadcast_to([P, U - SPLIT, 2]),
                                         scalar1=1.0, scalar2=-0.0, op0=mybir.AluOpType.mult, op1=mybir.AluOpType.add)
             elif t < 3:
                 nc.scalar.copy(out=right[:, :, t], in_=window[t][:, SPLIT:])

@@ -1,6 +1,7 @@
 from contextlib import ExitStack
 
 import concourse.mybir as mybir
+from concourse.masks import make_identity
 
 K, T, N, U = 512, 512, 512, 1024
 FLOPS = 2 * K * N * T
@@ -15,10 +16,11 @@ FP8X4 = mybir.dt.float8_e4m3fn_x4
 P = 128
 PACK = 4
 LIST = 16
+HALF = P // 2
 FIRST = 256
+QUARTER = 256
 SPLIT = 512
-BETWEEN = 192
-PIECE = 256
+SHARE = 40
 X_LOADS = ((0, FIRST), (FIRST, T))
 
 
@@ -31,47 +33,48 @@ def tile_picked_wkvput_none_lo_kernel(tc, x_words, x_scales, mem, w1, slot, out_
         offsets = keep.tile([P, T // LIST], U16, name="offsets")
         x_sc = keep.tile([P, T], U8, name="x_sc", align_bytes=64)
         x_part = [keep.tile([P, c1 - c0], I32, name="x_part%d" % c0, align_bytes=64) for c0, c1 in X_LOADS]
-        w_raw = [keep.tile([P, 2, N], F32, name="w_raw%d" % h) for h in range(2)]
+        w_raw = [keep.tile([P, PACK, N // 2], F32, name="w_raw%d" % h) for h in range(2)]
         window = [keep.tile([P, U], F32, name="window%d" % t) for t in range(PACK)]
+        ident = keep.tile([P, P], F32, name="ident")
+        nc.gpsimd.memset(x_sc[:].bitcast(I32), 0)
+        make_identity(nc, ident[:])
 
-        nc.vector.memset(x_sc[:].bitcast(I32), 0)
+        def rows_of(dram, t):
+            by_word = dram.rearrange("(l t) c -> l t c", t=PACK)
+            return by_word[t * HALF : (t + 1) * HALF, :2, :] if t < 2 else by_word[:, t, :]
+
         sc_rows = x_scales[0].bitcast(I32)
         w_rows = w1.rearrange("(p j) c -> p j c", j=PACK)
         x_cols = x_words[0].rearrange("p c r -> p (c r)").bitcast(I32)
-        mem_rows = mem.rearrange("(p t) c -> p t c", t=PACK)
-        out_rows = out_0.rearrange("(p t) c -> p t c", t=PACK)
-        nc.sync.dma_start(out=w_raw[0][:], in_=w_rows[:, :2, :])
-        nc.sync.dma_start(out=w_raw[1][:], in_=w_rows[:, 2:, :])
+        nc.sync.dma_start(offsets[:], slot)
+        nc.sync.dma_start(out=w_raw[0][:], in_=w_rows[:, :, : N // 2])
         for r in range(4):
             queue = nc.sync if r % 2 else nc.scalar
             queue.dma_start(out=x_sc[r:P:32, :].bitcast(I32), in_=sc_rows[r:16:4, :])
         nc.sync.dma_start(out=x_part[0][:], in_=x_cols[:, :FIRST])
-        nc.sync.dma_start(out=window[0][:], in_=mem_rows[:, 0, :])
-        nc.sync.dma_start(offsets[:], slot)
-        nc.sync.dma_start(out=window[1][:], in_=mem_rows[:, 1, :])
+        nc.sync.dma_start(out=window[0][:], in_=rows_of(mem, 0))
+        nc.sync.dma_start(out=w_raw[1][:], in_=w_rows[:, :, N // 2 :])
         nc.sync.dma_start(out=x_part[1][:], in_=x_cols[:, FIRST:])
-        for t in range(2, PACK):
-            nc.sync.dma_start(out=window[t][:], in_=mem_rows[:, t, :])
+        for t in range(1, PACK):
+            nc.sync.dma_start(out=window[t][:], in_=rows_of(mem, t))
 
         w_codes = keep.tile([P, N], I32, name="w_codes", align_bytes=64)
         w_sc = keep.tile([P, N], U8, name="w_sc", align_bytes=64)
-        src = [w_raw[h][:].rearrange("p j (m t) -> p m t j", t=PACK) for h in range(2)]
-        grouped = [keep.tile([P, P, PACK], BF16, name="grouped%d" % t, align_bytes=64) for t in range(PACK)]
+        src = [w_raw[h][:].rearrange("p j (l t) -> p l t j", t=PACK) for h in range(2)]
+        pairs = [keep.tile([P, HALF, 2, PACK], BF16, name="pairs%d" % h, align_bytes=64) for h in range(2)]
+        single = [keep.tile([P, 2, HALF, PACK], BF16, name="single%d" % h, align_bytes=64) for h in range(2)]
 
-        def deal(copy, t, h):
-            copy(out=grouped[t][:, :, 2 * h : 2 * h + 2], in_=src[h][:, :, t, :])
+        def quantize_w(c0, c1, grouped):
+            nc.vector.quantize_mx(out=w_codes[:, c0:c1].bitcast(FP8X4), scales=w_sc[:, c0:c1], in_=grouped)
 
-        def quantize_w(t):
-            rows = slice(t * P, (t + 1) * P)
-            nc.vector.quantize_mx(out=w_codes[:, rows].bitcast(FP8X4), scales=w_sc[:, rows], in_=grouped[t][:].rearrange("p m j -> p (m j)"))
+        def quantize_pairs(h):
+            quantize_w(h * P, (h + 1) * P, pairs[h][:].rearrange("p l e j -> p (l e j)"))
 
-        for h in range(2):
-            deal(nc.vector.tensor_copy, 0, h)
-            deal(nc.vector.tensor_copy, 1, h)
-            deal(nc.scalar.copy, 2, h)
-            deal(nc.scalar.copy, 3, h)
-        for t in range(PACK):
-            quantize_w(t)
+        def quantize_single(t, h):
+            quantize_w(t * P + h * HALF, t * P + (h + 1) * HALF, single[h][:, t - 2].rearrange("p l j -> p (l j)"))
+
+        def round_on_gpsimd(out, in_):
+            nc.gpsimd.tensor_scalar(out=out, in0=in_, scalar1=1.0, scalar2=-0.0, op0=mybir.AluOpType.mult, op1=mybir.AluOpType.add)
 
         def product(out, t, c0, c1):
             rows = slice(t * P, (t + 1) * P)
@@ -82,52 +85,90 @@ def tile_picked_wkvput_none_lo_kernel(tc, x_words, x_scales, mem, w1, slot, out_
                                 start=True, stop=True)
 
         y = [keep.tile([P, T], F32, name="y%d" % t) for t in range(PACK)]
-        for c0, c1 in X_LOADS:
-            for t in range(2):
-                step = P if (t, c0) == (0, 0) else c1 - c0
-                for d0 in range(c0, c1, step):
-                    acc = psum.tile([P, step], F32, name="acc%d_%d" % (t, d0))
-                    product(acc[:], t, d0, d0 + step)
-                    nc.scalar.copy(out=y[t][:, d0 : d0 + step], in_=acc[:])
-        for t in range(2, PACK):
-            acc = psum.tile([P, T], F32, name="acc%d" % t)
-            for c0, c1 in X_LOADS:
-                product(acc[:, c0:c1], t, c0, c1)
-            nc.scalar.copy(out=y[t][:], in_=acc[:])
+
+        def values(t, c0, c1, bank, copy=nc.scalar.copy):
+            acc = psum.tile([P, c1 - c0], F32, name="acc%d_%d" % (t, c0), tag="bank%d" % bank)
+            for d0, d1 in X_LOADS:
+                e0, e1 = max(c0, d0), min(c1, d1)
+                if e0 < e1:
+                    product(acc[:, e0 - c0 : e1 - c0], t, e0, e1)
+            copy(out=y[t][:, c0:c1], in_=acc[:])
 
         def scatter(t, c0, c1):
             nc.vector.tensor_copy(window[t][:].indirect(offsets[:, c0 // LIST : c1 // LIST]), y[t][:, c0:c1])
 
-        left = keep.tile([P, SPLIT, PACK], BF16, name="left", align_bytes=64)
-        right = keep.tile([P, U - SPLIT, PACK], BF16, name="right", align_bytes=64)
+        dealt = [single[h][:].rearrange("p t l j -> p l t j") for h in range(2)]
+        nc.vector.tensor_copy(out=pairs[0][:, :SHARE], in_=src[0][:, :SHARE, :2, :])
+        nc.scalar.copy(out=pairs[0][:, SHARE:], in_=src[0][:, SHARE:, :2, :])
+        quantize_pairs(0)
+        nc.scalar.copy(out=dealt[0], in_=src[0][:, :, 2:, :])
+        quantize_single(2, 0)
+        quantize_single(3, 0)
+        values(0, 0, P, 0)
+        values(0, P, FIRST, 1, nc.vector.tensor_copy)
         scatter(0, 0, FIRST)
-        scatter(1, 0, BETWEEN)
-        for t in range(PACK):
-            scatter(t, (FIRST, BETWEEN, 0, 0)[t], T)
-            nc.sync.dma_start(out=out_rows[:, t, :], in_=window[t][:])
-            if t < 2:
-                nc.scalar.copy(out=left[:, :, t], in_=window[t][:, :SPLIT])
-            elif t == 2:
-                nc.gpsimd.tensor_scalar(out=left[:, :, t:], in0=window[t][:, :SPLIT].unsqueeze(2).broadcast_to([P, SPLIT, 2]),
-                                        scalar1=1.0, scalar2=-0.0, op0=mybir.AluOpType.mult, op1=mybir.AluOpType.add)
-            else:
-                for c0 in range(0, SPLIT, PIECE):
-                    nc.vector.tensor_copy(out=left[:, c0 : c0 + PIECE, t], in_=window[t][:, c0 : c0 + PIECE])
-            if t == 0:
-                nc.gpsimd.tensor_scalar(out=right[:, :, t : t + 2], in0=window[t][:, SPLIT:].unsqueeze(2).broadcast_to([P, U - SPLIT, 2]),
-                                        scalar1=1.0, scalar2=-0.0, op0=mybir.AluOpType.mult, op1=mybir.AluOpType.add)
-            elif t < 3:
-                nc.scalar.copy(out=right[:, :, t], in_=window[t][:, SPLIT:])
-            else:
-                for c0, c1 in ((0, 256), (256, 384), (384, 512)):
-                    nc.scalar.copy(out=right[:, c0:c1, t], in_=window[t][:, SPLIT + c0 : SPLIT + c1])
+        nc.scalar.copy(out=pairs[1][:], in_=src[1][:, :, :2, :])
+        round_on_gpsimd(dealt[1], src[1][:, :, 2:, :])
+        quantize_pairs(1)
+        quantize_single(2, 1)
+        quantize_single(3, 1)
+        values(0, FIRST, T, 2)
+        scatter(0, FIRST, T)
+        values(1, 0, T, 3)
+        values(2, 0, T, 4)
+        values(3, 0, T, 5)
+
+        turned = [keep.tile([P, 2, 2, P], BF16, name="turned%d" % b) for b in range(U // QUARTER)]
+        halves = [keep.tile([P, SPLIT, PACK], BF16, name="half%d" % b, align_bytes=64) for b in range(2)]
+
+        def side(c0, c1):
+            return halves[c0 // SPLIT][:, c0 % SPLIT : c0 % SPLIT + c1 - c0, :]
+
+
+        def turn(t, b, bank):
+            across = psum.tile([P, 2, P], F32, name="across%d_%d" % (t, b), tag="bank%d" % bank)
+            for i in range(2):
+                c0 = b * QUARTER + i * P
+                nc.tensor.transpose(across[:, i, :], window[t][:, c0 : c0 + P], ident[:])
+            nc.scalar.copy(out=turned[b][:, :, t, :], in_=across[:])
+
+        def turn_back(b, bank):
+            back = psum.tile([P, QUARTER], F32, name="back%d" % b, tag="bank%d" % bank)
+            words = turned[b][:].rearrange("p i h q -> p (i h q)").bitcast(F32)
+            for i in range(2):
+                nc.tensor.transpose(back[:, i * P : (i + 1) * P], words[:, i * P : (i + 1) * P], ident[:])
+            both = side(b * QUARTER, (b + 1) * QUARTER).rearrange("p c t -> p (c t)").bitcast(F32).rearrange("p (c u) -> p c u", u=2)
+            nc.scalar.copy(out=both, in_=back[:].unsqueeze(2).broadcast_to([P, QUARTER, 2]))
+
+        nc.sync.dma_start(out=rows_of(out_0, 0), in_=window[0][:])
+        for b in range(U // QUARTER):
+            turn(0, b, 4 + b % 2)
+        scatter(1, 0, T)
+        nc.sync.dma_start(out=rows_of(out_0, 1), in_=window[1][:])
+        for b in range(U // QUARTER + 1):
+            if b < U // QUARTER:
+                turn(1, b, 4 + b % 2)
+            if b > 0:
+                turn_back(b - 1, b - 1)
+
+        scatter(2, 0, T)
+        nc.sync.dma_start(out=rows_of(out_0, 2), in_=window[2][:])
+        round_on_gpsimd(side(0, SPLIT)[:, :, 2:], window[2][:, :SPLIT].unsqueeze(2).broadcast_to([P, SPLIT, 2]))
+        for c0 in range(SPLIT, U, QUARTER):
+            nc.scalar.copy(out=side(c0, c0 + QUARTER)[:, :, 2], in_=window[2][:, c0 : c0 + QUARTER])
+        scatter(3, 0, T)
+        nc.sync.dma_start(out=rows_of(out_0, 3), in_=window[3][:])
+        for c0 in range(0, SPLIT, QUARTER):
+            nc.vector.tensor_copy(out=side(c0, c0 + QUARTER)[:, :, 3], in_=window[3][:, c0 : c0 + QUARTER])
+        for c0, c1 in ((512, 768), (768, 896), (896, 1024)):
+            nc.scalar.copy(out=side(c0, c1)[:, :, 3], in_=window[3][:, c0:c1])
 
         o_sc = keep.tile([P, U], U8, name="o_sc", align_bytes=64)
         o_codes = keep.tile([P, U], I32, name="o_codes", align_bytes=64)
         o_words = out_1[0].rearrange("p c r -> p (c r)").bitcast(I32)
         stored = 0
         for c0, c1 in ((0, 256), (256, 384), (384, 512), (512, 768), (768, 896), (896, 1024)):
-            part = left[:, c0:c1, :] if c0 < SPLIT else right[:, c0 - SPLIT : c1 - SPLIT, :]
+            part = side(c0, c1)
             nc.vector.quantize_mx(out=o_codes[:, c0:c1].bitcast(FP8X4), scales=o_sc[:, c0:c1], in_=part.rearrange("p c t -> p (c t)"))
             if c1 in (384, 768, 1024):
                 nc.sync.dma_start(out=o_words[:, stored:c1], in_=o_codes[:, stored:c1])

@@ -20,8 +20,8 @@ HALF = P // 2
 FIRST = 256
 QUARTER = 256
 SPLIT = 512
-SHARE = 40
-X_LOADS = ((0, FIRST), (FIRST, T))
+SHARE = 32
+PARTS = ((0, 512), (512, 768), (768, 896), (896, 1024))
 
 
 def tile_picked_wkvput_none_lo_kernel(tc, x_words, x_scales, mem, w1, slot, out_0, out_1, out_2):
@@ -32,7 +32,7 @@ def tile_picked_wkvput_none_lo_kernel(tc, x_words, x_scales, mem, w1, slot, out_
 
         offsets = keep.tile([P, T // LIST], U16, name="offsets")
         x_sc = keep.tile([P, T], U8, name="x_sc", align_bytes=64)
-        x_part = [keep.tile([P, c1 - c0], I32, name="x_part%d" % c0, align_bytes=64) for c0, c1 in X_LOADS]
+        x_codes = keep.tile([P, T], I32, name="x_codes", align_bytes=64)
         w_raw = [keep.tile([P, PACK, N // 2], F32, name="w_raw%d" % h) for h in range(2)]
         window = [keep.tile([P, U], F32, name="window%d" % t) for t in range(PACK)]
         ident = keep.tile([P, P], F32, name="ident")
@@ -51,10 +51,10 @@ def tile_picked_wkvput_none_lo_kernel(tc, x_words, x_scales, mem, w1, slot, out_
         for r in range(4):
             queue = nc.sync if r % 2 else nc.scalar
             queue.dma_start(out=x_sc[r:P:32, :].bitcast(I32), in_=sc_rows[r:16:4, :])
-        nc.sync.dma_start(out=x_part[0][:], in_=x_cols[:, :FIRST])
+        nc.sync.dma_start(out=x_codes[:, :FIRST], in_=x_cols[:, :FIRST])
         nc.sync.dma_start(out=window[0][:], in_=rows_of(mem, 0))
         nc.sync.dma_start(out=w_raw[1][:], in_=w_rows[:, :, N // 2 :])
-        nc.sync.dma_start(out=x_part[1][:], in_=x_cols[:, FIRST:])
+        nc.sync.dma_start(out=x_codes[:, FIRST:], in_=x_cols[:, FIRST:])
         for t in range(1, PACK):
             nc.sync.dma_start(out=window[t][:], in_=rows_of(mem, t))
 
@@ -62,7 +62,6 @@ def tile_picked_wkvput_none_lo_kernel(tc, x_words, x_scales, mem, w1, slot, out_
         w_sc = keep.tile([P, N], U8, name="w_sc", align_bytes=64)
         src = [w_raw[h][:].rearrange("p j (l t) -> p l t j", t=PACK) for h in range(2)]
         pairs = [keep.tile([P, HALF, 2, PACK], BF16, name="pairs%d" % h, align_bytes=64) for h in range(2)]
-        single = [keep.tile([P, 2, HALF, PACK], BF16, name="single%d" % h, align_bytes=64) for h in range(2)]
 
         def quantize_w(c0, c1, grouped):
             nc.vector.quantize_mx(out=w_codes[:, c0:c1].bitcast(FP8X4), scales=w_sc[:, c0:c1], in_=grouped)
@@ -70,59 +69,57 @@ def tile_picked_wkvput_none_lo_kernel(tc, x_words, x_scales, mem, w1, slot, out_
         def quantize_pairs(h):
             quantize_w(h * P, (h + 1) * P, pairs[h][:].rearrange("p l e j -> p (l e j)"))
 
-        def quantize_single(t, h):
-            quantize_w(t * P + h * HALF, t * P + (h + 1) * HALF, single[h][:, t - 2].rearrange("p l j -> p (l j)"))
+        def singles(h, copy, tag):
+            single = keep.tile([P, 2, HALF, PACK], BF16, name="single%d" % h, tag=tag, align_bytes=64)
+            for t in range(2, PACK):
+                copy(out=single[:, t - 2], in_=src[h][:, :, t, :])
+            for t in range(2, PACK):
+                quantize_w(t * P + h * HALF, t * P + (h + 1) * HALF, single[:, t - 2].rearrange("p l j -> p (l j)"))
 
         def round_on_gpsimd(out, in_):
             nc.gpsimd.tensor_scalar(out=out, in0=in_, scalar1=1.0, scalar2=-0.0, op0=mybir.AluOpType.mult, op1=mybir.AluOpType.add)
 
         def product(out, t, c0, c1):
             rows = slice(t * P, (t + 1) * P)
-            h = 0 if c0 < FIRST else 1
-            base = X_LOADS[h][0]
             nc.tensor.matmul_mx(out=out, lhsT=w_codes[:, rows].bitcast(FP8X4), lhsT_scale=w_sc[:, rows],
-                                rhs=x_part[h][:, c0 - base : c1 - base].bitcast(FP8X4), rhs_scale=x_sc[:, c0:c1],
+                                rhs=x_codes[:, c0:c1].bitcast(FP8X4), rhs_scale=x_sc[:, c0:c1],
                                 start=True, stop=True)
 
         y = [keep.tile([P, T], F32, name="y%d" % t) for t in range(PACK)]
 
-        def values(t, c0, c1, bank, copy=nc.scalar.copy):
+        def values(t, cuts, bank):
+            c0, c1 = cuts[0], cuts[-1]
             acc = psum.tile([P, c1 - c0], F32, name="acc%d_%d" % (t, c0), tag="bank%d" % bank)
-            for d0, d1 in X_LOADS:
-                e0, e1 = max(c0, d0), min(c1, d1)
-                if e0 < e1:
-                    product(acc[:, e0 - c0 : e1 - c0], t, e0, e1)
-            copy(out=y[t][:, c0:c1], in_=acc[:])
+            for e0, e1 in zip(cuts, cuts[1:]):
+                product(acc[:, e0 - c0 : e1 - c0], t, e0, e1)
+            nc.scalar.copy(out=y[t][:, c0:c1], in_=acc[:])
 
         def scatter(t, c0, c1):
             nc.vector.tensor_copy(window[t][:].indirect(offsets[:, c0 // LIST : c1 // LIST]), y[t][:, c0:c1])
 
-        dealt = [single[h][:].rearrange("p t l j -> p l t j") for h in range(2)]
         nc.vector.tensor_copy(out=pairs[0][:, :SHARE], in_=src[0][:, :SHARE, :2, :])
         nc.scalar.copy(out=pairs[0][:, SHARE:], in_=src[0][:, SHARE:, :2, :])
         quantize_pairs(0)
-        nc.scalar.copy(out=dealt[0], in_=src[0][:, :, 2:, :])
-        quantize_single(2, 0)
-        quantize_single(3, 0)
-        values(0, 0, P, 0)
-        values(0, P, FIRST, 1, nc.vector.tensor_copy)
+        singles(0, nc.vector.tensor_copy, "pairs0")
+        values(0, (0, P), 0)
+        values(0, (P, FIRST), 1)
         scatter(0, 0, FIRST)
         nc.scalar.copy(out=pairs[1][:], in_=src[1][:, :, :2, :])
-        round_on_gpsimd(dealt[1], src[1][:, :, 2:, :])
         quantize_pairs(1)
-        quantize_single(2, 1)
-        quantize_single(3, 1)
-        values(0, FIRST, T, 2)
+        values(0, (FIRST, T), 2)
+        singles(1, round_on_gpsimd, "high")
         scatter(0, FIRST, T)
-        values(1, 0, T, 3)
-        values(2, 0, T, 4)
-        values(3, 0, T, 5)
+        values(1, (0, T // 2), 3)
+        values(1, (T // 2, T), 7)
+        values(2, (0, T), 4)
+        values(3, (0, T), 5)
 
         turned = [keep.tile([P, 2, 2, P], BF16, name="turned%d" % b) for b in range(U // QUARTER)]
-        halves = [keep.tile([P, SPLIT, PACK], BF16, name="half%d" % b, align_bytes=64) for b in range(2)]
+        parts = {c0: keep.tile([P, c1 - c0, PACK], BF16, name="part%d" % c0, align_bytes=64) for c0, c1 in PARTS}
 
         def side(c0, c1):
-            return halves[c0 // SPLIT][:, c0 % SPLIT : c0 % SPLIT + c1 - c0, :]
+            base = max(d0 for d0, d1 in PARTS if d0 <= c0)
+            return parts[base][:, c0 - base : c1 - base, :]
 
 
         def turn(t, b, bank):
@@ -137,30 +134,35 @@ def tile_picked_wkvput_none_lo_kernel(tc, x_words, x_scales, mem, w1, slot, out_
             words = turned[b][:].rearrange("p i h q -> p (i h q)").bitcast(F32)
             for i in range(2):
                 nc.tensor.transpose(back[:, i * P : (i + 1) * P], words[:, i * P : (i + 1) * P], ident[:])
-            both = side(b * QUARTER, (b + 1) * QUARTER).rearrange("p c t -> p (c t)").bitcast(F32).rearrange("p (c u) -> p c u", u=2)
-            nc.scalar.copy(out=both, in_=back[:].unsqueeze(2).broadcast_to([P, QUARTER, 2]))
+            base = b * QUARTER
+            for d0, d1 in PARTS:
+                c0, c1 = max(d0, base), min(d1, base + QUARTER)
+                if c0 < c1:
+                    both = side(c0, c1).rearrange("p c t -> p (c t)").bitcast(F32).rearrange("p (c u) -> p c u", u=2)
+                    nc.scalar.copy(out=both, in_=back[:, c0 - base : c1 - base].unsqueeze(2).broadcast_to([P, c1 - c0, 2]))
 
         nc.sync.dma_start(out=rows_of(out_0, 0), in_=window[0][:])
         for b in range(U // QUARTER):
-            turn(0, b, 4 + b % 2)
+            turn(0, b, (3, 7, 4, 5)[b])
         scatter(1, 0, T)
         nc.sync.dma_start(out=rows_of(out_0, 1), in_=window[1][:])
         for b in range(U // QUARTER + 1):
             if b < U // QUARTER:
-                turn(1, b, 4 + b % 2)
+                turn(1, b, 5 - b % 2)
             if b > 0:
                 turn_back(b - 1, b - 1)
 
         scatter(2, 0, T)
         nc.sync.dma_start(out=rows_of(out_0, 2), in_=window[2][:])
-        round_on_gpsimd(side(0, SPLIT)[:, :, 2:], window[2][:, :SPLIT].unsqueeze(2).broadcast_to([P, SPLIT, 2]))
-        for c0 in range(SPLIT, U, QUARTER):
-            nc.scalar.copy(out=side(c0, c0 + QUARTER)[:, :, 2], in_=window[2][:, c0 : c0 + QUARTER])
+        for c0, c1 in (PARTS[0], PARTS[3]):
+            round_on_gpsimd(side(c0, c1)[:, :, 2:], window[2][:, c0:c1].unsqueeze(2).broadcast_to([P, c1 - c0, 2]))
+        for c0, c1 in PARTS[1:3]:
+            nc.scalar.copy(out=side(c0, c1)[:, :, 2], in_=window[2][:, c0:c1])
         scatter(3, 0, T)
         nc.sync.dma_start(out=rows_of(out_0, 3), in_=window[3][:])
         for c0 in range(0, SPLIT, QUARTER):
             nc.vector.tensor_copy(out=side(c0, c0 + QUARTER)[:, :, 3], in_=window[3][:, c0 : c0 + QUARTER])
-        for c0, c1 in ((512, 768), (768, 896), (896, 1024)):
+        for c0, c1 in PARTS[1:]:
             nc.scalar.copy(out=side(c0, c1)[:, :, 3], in_=window[3][:, c0:c1])
 
         o_sc = keep.tile([P, U], U8, name="o_sc", align_bytes=64)

@@ -1,7 +1,6 @@
 from contextlib import ExitStack
 
 import concourse.mybir as mybir
-from concourse.masks import make_identity
 
 K, T, N, U = 512, 512, 512, 1024
 FLOPS = 2 * K * N * T
@@ -9,19 +8,20 @@ FLOPS = 2 * K * N * T
 F32 = mybir.dt.float32
 BF16 = mybir.dt.bfloat16
 I32 = mybir.dt.int32
+U32 = mybir.dt.uint32
 U16 = mybir.dt.uint16
 U8 = mybir.dt.uint8
 FP8X4 = mybir.dt.float8_e4m3fn_x4
+COPY = mybir.ActivationFunctionType.Copy
 
 P = 128
 PACK = 4
 LIST = 16
-HALF = P // 2
-FIRST = 256
-QUARTER = 256
+HALF = 256
 SPLIT = 512
-SHARE = 32
-PARTS = ((0, 512), (512, 768), (768, 896), (896, 1024))
+ON_VECTOR = ((0, 256), (256, SPLIT))
+ON_SCALAR = ((SPLIT, 768), (768, 896), (896, 1024))
+STORED = (256, 768, 1024)
 
 
 def tile_picked_wkvput_none_lo_kernel(tc, x_words, x_scales, mem, w1, slot, out_0, out_1, out_2):
@@ -35,144 +35,113 @@ def tile_picked_wkvput_none_lo_kernel(tc, x_words, x_scales, mem, w1, slot, out_
         x_codes = keep.tile([P, T], I32, name="x_codes", align_bytes=64)
         w_raw = [keep.tile([P, PACK, N // 2], F32, name="w_raw%d" % h) for h in range(2)]
         window = [keep.tile([P, U], F32, name="window%d" % t) for t in range(PACK)]
-        ident = keep.tile([P, P], F32, name="ident")
         nc.gpsimd.memset(x_sc[:].bitcast(I32), 0)
-        make_identity(nc, ident[:])
 
         def rows_of(dram, t):
-            by_word = dram.rearrange("(l t) c -> l t c", t=PACK)
-            return by_word[t * HALF : (t + 1) * HALF, :2, :] if t < 2 else by_word[:, t, :]
+            return dram.rearrange("(l t) c -> l t c", t=PACK)[:, t, :]
 
         sc_rows = x_scales[0].bitcast(I32)
         w_rows = w1.rearrange("(p j) c -> p j c", j=PACK)
         x_cols = x_words[0].rearrange("p c r -> p (c r)").bitcast(I32)
         nc.sync.dma_start(offsets[:], slot)
         nc.sync.dma_start(out=w_raw[0][:], in_=w_rows[:, :, : N // 2])
+        nc.sync.dma_start(out=w_raw[1][:], in_=w_rows[:, :, N // 2 :])
         for r in range(4):
             queue = nc.sync if r % 2 else nc.scalar
             queue.dma_start(out=x_sc[r:P:32, :].bitcast(I32), in_=sc_rows[r:16:4, :])
-        nc.sync.dma_start(out=x_codes[:, :FIRST], in_=x_cols[:, :FIRST])
-        nc.sync.dma_start(out=window[0][:], in_=rows_of(mem, 0))
-        nc.sync.dma_start(out=w_raw[1][:], in_=w_rows[:, :, N // 2 :])
-        nc.sync.dma_start(out=x_codes[:, FIRST:], in_=x_cols[:, FIRST:])
-        for t in range(1, PACK):
+        nc.sync.dma_start(out=x_codes[:], in_=x_cols)
+        for t in range(2):
             nc.sync.dma_start(out=window[t][:], in_=rows_of(mem, t))
+        nc.sync.dma_start(out=window[3][:, : U // 2], in_=rows_of(mem, 3)[:, : U // 2])
+        nc.sync.dma_start(out=window[2][:], in_=rows_of(mem, 2))
+        nc.sync.dma_start(out=window[3][:, U // 2 :], in_=rows_of(mem, 3)[:, U // 2 :])
 
         w_codes = keep.tile([P, N], I32, name="w_codes", align_bytes=64)
         w_sc = keep.tile([P, N], U8, name="w_sc", align_bytes=64)
-        src = [w_raw[h][:].rearrange("p j (l t) -> p l t j", t=PACK) for h in range(2)]
-        pairs = [keep.tile([P, HALF, 2, PACK], BF16, name="pairs%d" % h, align_bytes=64) for h in range(2)]
+        grouped = [keep.tile([P, P, PACK], BF16, name="grouped%d" % t, align_bytes=64) for t in range(PACK)]
+        for h in range(2):
+            src = w_raw[h][:].rearrange("p j (l t) -> p l j t", t=PACK)
+            for t in range(PACK):
+                copy = nc.vector.tensor_copy if t < 2 else nc.scalar.copy
+                copy(out=grouped[t][:, h * P // 2 : (h + 1) * P // 2, :], in_=src[:, :, :, t])
+        for t in range(PACK):
+            nc.vector.quantize_mx(out=w_codes[:, t * P : (t + 1) * P].bitcast(FP8X4), scales=w_sc[:, t * P : (t + 1) * P],
+                                  in_=grouped[t][:].rearrange("p l j -> p (l j)"))
 
-        def quantize_w(c0, c1, grouped):
-            nc.vector.quantize_mx(out=w_codes[:, c0:c1].bitcast(FP8X4), scales=w_sc[:, c0:c1], in_=grouped)
+        y = [keep.tile([P, T], F32, name="y%d" % t) for t in range(PACK)]
 
-        def quantize_pairs(h):
-            quantize_w(h * P, (h + 1) * P, pairs[h][:].rearrange("p l e j -> p (l e j)"))
+        def values(t, c0, c1, copy):
+            acc = psum.tile([P, c1 - c0], F32, name="acc%d_%d" % (t, c0))
+            rows = slice(t * P, (t + 1) * P)
+            nc.tensor.matmul_mx(out=acc[:], lhsT=w_codes[:, rows].bitcast(FP8X4), lhsT_scale=w_sc[:, rows],
+                                rhs=x_codes[:, c0:c1].bitcast(FP8X4), rhs_scale=x_sc[:, c0:c1],
+                                start=True, stop=True)
+            copy(out=y[t][:, c0:c1], in_=acc[:])
 
-        def singles(h, copy, tag):
-            single = keep.tile([P, 2, HALF, PACK], BF16, name="single%d" % h, tag=tag, align_bytes=64)
-            for t in range(2, PACK):
-                copy(out=single[:, t - 2], in_=src[h][:, :, t, :])
-            for t in range(2, PACK):
-                quantize_w(t * P + h * HALF, t * P + (h + 1) * HALF, single[:, t - 2].rearrange("p l j -> p (l j)"))
+        def scatter(t, c0, c1):
+            target = window[t][:].indirect(offsets[:, c0 // LIST : c1 // LIST])
+            if t % 2:
+                nc.vector.tensor_copy(target, y[t][:, c0:c1])
+            else:
+                nc.scalar.activation(target, y[t][:, c0:c1], COPY)
 
         def round_on_gpsimd(out, in_):
             nc.gpsimd.tensor_scalar(out=out, in0=in_, scalar1=1.0, scalar2=-0.0, op0=mybir.AluOpType.mult, op1=mybir.AluOpType.add)
 
-        def product(out, t, c0, c1):
-            rows = slice(t * P, (t + 1) * P)
-            nc.tensor.matmul_mx(out=out, lhsT=w_codes[:, rows].bitcast(FP8X4), lhsT_scale=w_sc[:, rows],
-                                rhs=x_codes[:, c0:c1].bitcast(FP8X4), rhs_scale=x_sc[:, c0:c1],
-                                start=True, stop=True)
+        sides = ((0, SPLIT), (SPLIT, U))
+        pairs = [keep.tile([P, (c1 - c0) * PACK], BF16, name="pairs%d" % c0) for c0, c1 in sides]
+        lined = {c0: keep.tile([P, (c1 - c0) * PACK], BF16, name="lined%d" % c0, align_bytes=64) for c0, c1 in ON_VECTOR + ON_SCALAR}
 
-        y = [keep.tile([P, T], F32, name="y%d" % t) for t in range(PACK)]
+        def pairs_of(view, c0, c1):
+            side = int(c0 >= SPLIT)
+            base = sides[side][0]
+            return view(pairs[side][:])[:, :, c0 - base : c1 - base]
 
-        def values(t, cuts, bank):
-            c0, c1 = cuts[0], cuts[-1]
-            acc = psum.tile([P, c1 - c0], F32, name="acc%d_%d" % (t, c0), tag="bank%d" % bank)
-            for e0, e1 in zip(cuts, cuts[1:]):
-                product(acc[:, e0 - c0 : e1 - c0], t, e0, e1)
-            nc.scalar.copy(out=y[t][:, c0:c1], in_=acc[:])
+        def round_place(copy, t, c0, c1):
+            places = pairs_of(lambda ap: ap.rearrange("p (u c e) -> p u c e", u=2, e=2), c0, c1)
+            copy(out=places[:, t // 2, :, t % 2], in_=window[t][:, c0:c1])
 
-        def scatter(t, c0, c1):
-            nc.vector.tensor_copy(window[t][:].indirect(offsets[:, c0 // LIST : c1 // LIST]), y[t][:, c0:c1])
+        def line_up(copy, kind, c0, c1):
+            words = pairs_of(lambda ap: ap.bitcast(kind).rearrange("p (u c) -> p u c", u=2), c0, c1)
+            copy(out=lined[c0][:].bitcast(kind).rearrange("p (c u) -> p c u", u=2), in_=words.rearrange("p u c -> p c u"))
 
-        nc.vector.tensor_copy(out=pairs[0][:, :SHARE], in_=src[0][:, :SHARE, :2, :])
-        nc.scalar.copy(out=pairs[0][:, SHARE:], in_=src[0][:, SHARE:, :2, :])
-        quantize_pairs(0)
-        singles(0, nc.vector.tensor_copy, "pairs0")
-        values(0, (0, P), 0)
-        values(0, (P, FIRST), 1)
-        scatter(0, 0, FIRST)
-        nc.scalar.copy(out=pairs[1][:], in_=src[1][:, :, :2, :])
-        quantize_pairs(1)
-        values(0, (FIRST, T), 2)
-        singles(1, round_on_gpsimd, "high")
-        scatter(0, FIRST, T)
-        values(1, (0, T // 2), 3)
-        values(1, (T // 2, T), 7)
-        values(2, (0, T), 4)
-        values(3, (0, T), 5)
-
-        turned = [keep.tile([P, 2, 2, P], BF16, name="turned%d" % b) for b in range(U // QUARTER)]
-        parts = {c0: keep.tile([P, c1 - c0, PACK], BF16, name="part%d" % c0, align_bytes=64) for c0, c1 in PARTS}
-
-        def side(c0, c1):
-            base = max(d0 for d0, d1 in PARTS if d0 <= c0)
-            return parts[base][:, c0 - base : c1 - base, :]
-
-
-        def turn(t, b, bank):
-            across = psum.tile([P, 2, P], F32, name="across%d_%d" % (t, b), tag="bank%d" % bank)
-            for i in range(2):
-                c0 = b * QUARTER + i * P
-                nc.tensor.transpose(across[:, i, :], window[t][:, c0 : c0 + P], ident[:])
-            nc.scalar.copy(out=turned[b][:, :, t, :], in_=across[:])
-
-        def turn_back(b, bank):
-            back = psum.tile([P, QUARTER], F32, name="back%d" % b, tag="bank%d" % bank)
-            words = turned[b][:].rearrange("p i h q -> p (i h q)").bitcast(F32)
-            for i in range(2):
-                nc.tensor.transpose(back[:, i * P : (i + 1) * P], words[:, i * P : (i + 1) * P], ident[:])
-            base = b * QUARTER
-            for d0, d1 in PARTS:
-                c0, c1 = max(d0, base), min(d1, base + QUARTER)
-                if c0 < c1:
-                    both = side(c0, c1).rearrange("p c t -> p (c t)").bitcast(F32).rearrange("p (c u) -> p c u", u=2)
-                    nc.scalar.copy(out=both, in_=back[:, c0 - base : c1 - base].unsqueeze(2).broadcast_to([P, c1 - c0, 2]))
-
-        nc.sync.dma_start(out=rows_of(out_0, 0), in_=window[0][:])
-        for b in range(U // QUARTER):
-            turn(0, b, (3, 7, 4, 5)[b])
+        values(0, 0, HALF, nc.vector.tensor_copy)
+        scatter(0, 0, HALF)
+        values(1, 0, HALF, nc.vector.tensor_copy)
+        values(1, HALF, T, nc.vector.tensor_copy)
+        values(0, HALF, T, nc.vector.tensor_copy)
+        values(2, 0, HALF, nc.scalar.copy)
+        values(2, HALF, T, nc.scalar.copy)
+        scatter(0, HALF, T)
         scatter(1, 0, T)
-        nc.sync.dma_start(out=rows_of(out_0, 1), in_=window[1][:])
-        for b in range(U // QUARTER + 1):
-            if b < U // QUARTER:
-                turn(1, b, 5 - b % 2)
-            if b > 0:
-                turn_back(b - 1, b - 1)
-
-        scatter(2, 0, T)
-        nc.sync.dma_start(out=rows_of(out_0, 2), in_=window[2][:])
-        for c0, c1 in (PARTS[0], PARTS[3]):
-            round_on_gpsimd(side(c0, c1)[:, :, 2:], window[2][:, c0:c1].unsqueeze(2).broadcast_to([P, c1 - c0, 2]))
-        for c0, c1 in PARTS[1:3]:
-            nc.scalar.copy(out=side(c0, c1)[:, :, 2], in_=window[2][:, c0:c1])
+        for t in range(2):
+            nc.sync.dma_start(out=rows_of(out_0, t), in_=window[t][:])
+            for c0, c1 in sides:
+                round_place(round_on_gpsimd, t, c0, c1)
+        values(3, 0, T, nc.vector.tensor_copy)
         scatter(3, 0, T)
-        nc.sync.dma_start(out=rows_of(out_0, 3), in_=window[3][:])
-        for c0 in range(0, SPLIT, QUARTER):
-            nc.vector.tensor_copy(out=side(c0, c0 + QUARTER)[:, :, 3], in_=window[3][:, c0 : c0 + QUARTER])
-        for c0, c1 in PARTS[1:]:
-            nc.scalar.copy(out=side(c0, c1)[:, :, 3], in_=window[3][:, c0:c1])
+        scatter(2, 0, HALF)
+        scatter(2, HALF, T)
+        for t in (2, 3):
+            nc.sync.dma_start(out=rows_of(out_0, t), in_=window[t][:])
+        round_place(nc.scalar.copy, 2, SPLIT, U)
+        round_place(nc.vector.tensor_copy, 2, 0, SPLIT)
+        for c0, c1 in ON_VECTOR:
+            round_place(nc.vector.tensor_copy, 3, c0, c1)
+        for c0, c1 in ON_VECTOR:
+            line_up(nc.vector.tensor_copy, I32, c0, c1)
+        for c0, c1 in ON_SCALAR:
+            round_place(nc.scalar.copy, 3, c0, c1)
+        for c0, c1 in ON_SCALAR:
+            line_up(nc.scalar.copy, U32, c0, c1)
 
         o_sc = keep.tile([P, U], U8, name="o_sc", align_bytes=64)
         o_codes = keep.tile([P, U], I32, name="o_codes", align_bytes=64)
         o_words = out_1[0].rearrange("p c r -> p (c r)").bitcast(I32)
         stored = 0
-        for c0, c1 in ((0, 256), (256, 384), (384, 512), (512, 768), (768, 896), (896, 1024)):
-            part = side(c0, c1)
-            nc.vector.quantize_mx(out=o_codes[:, c0:c1].bitcast(FP8X4), scales=o_sc[:, c0:c1], in_=part.rearrange("p c t -> p (c t)"))
-            if c1 in (384, 768, 1024):
+        for c0, c1 in ON_VECTOR + ON_SCALAR:
+            nc.vector.quantize_mx(out=o_codes[:, c0:c1].bitcast(FP8X4), scales=o_sc[:, c0:c1], in_=lined[c0][:])
+            if c1 in STORED:
                 nc.sync.dma_start(out=o_words[:, stored:c1], in_=o_codes[:, stored:c1])
                 stored = c1
         o_rows = out_2[0].bitcast(I32)

@@ -21,7 +21,7 @@ HALF = 256
 SPLIT = 512
 ON_VECTOR = ((0, 256), (256, SPLIT))
 ON_SCALAR = ((SPLIT, 768), (768, 896), (896, 1024))
-STORED = (256, 768, 1024)
+STORED = (512, 768, 1024)
 
 
 def tile_picked_wkvput_none_lo_kernel(tc, x_words, x_scales, mem, w1, slot, out_0, out_1, out_2):
@@ -50,52 +50,49 @@ def tile_picked_wkvput_none_lo_kernel(tc, x_words, x_scales, mem, w1, slot, out_
             queue = nc.sync if r % 2 else nc.scalar
             queue.dma_start(out=x_sc[r:P:32, :].bitcast(I32), in_=sc_rows[r:16:4, :])
         nc.sync.dma_start(out=x_codes[:], in_=x_cols)
-        for t in range(2):
+        for t in range(PACK):
             nc.sync.dma_start(out=window[t][:], in_=rows_of(mem, t))
-        nc.sync.dma_start(out=window[3][:, : U // 2], in_=rows_of(mem, 3)[:, : U // 2])
-        nc.sync.dma_start(out=window[2][:], in_=rows_of(mem, 2))
-        nc.sync.dma_start(out=window[3][:, U // 2 :], in_=rows_of(mem, 3)[:, U // 2 :])
 
         w_codes = keep.tile([P, N], I32, name="w_codes", align_bytes=64)
         w_sc = keep.tile([P, N], U8, name="w_sc", align_bytes=64)
-        grouped = [keep.tile([P, P, PACK], BF16, name="grouped%d" % t, align_bytes=64) for t in range(PACK)]
+        grouped = [keep.tile([P, 2, P, PACK], BF16, name="grouped%d" % u, align_bytes=64) for u in range(2)]
         for h in range(2):
             src = w_raw[h][:].rearrange("p j (l t) -> p l j t", t=PACK)
-            for t in range(PACK):
-                copy = nc.vector.tensor_copy if t < 2 else nc.scalar.copy
-                copy(out=grouped[t][:, h * P // 2 : (h + 1) * P // 2, :], in_=src[:, :, :, t])
+            for u, copy in enumerate((nc.vector.tensor_copy, nc.scalar.copy)):
+                dst = grouped[u][:, :, h * P // 2 : (h + 1) * P // 2, :].rearrange("p e l j -> p l j e")
+                copy(out=dst, in_=src[:, :, :, 2 * u : 2 * u + 2])
         for t in range(PACK):
             nc.vector.quantize_mx(out=w_codes[:, t * P : (t + 1) * P].bitcast(FP8X4), scales=w_sc[:, t * P : (t + 1) * P],
-                                  in_=grouped[t][:].rearrange("p l j -> p (l j)"))
+                                  in_=grouped[t // 2][:, t % 2].rearrange("p l j -> p (l j)"))
 
-        y = [keep.tile([P, T], F32, name="y%d" % t) for t in range(PACK)]
+        def values(name, pieces, copy, out):
+            acc = psum.tile([P, sum(c1 - c0 for t, c0, c1 in pieces)], F32, name=name)
+            at = 0
+            for t, c0, c1 in pieces:
+                rows = slice(t * P, (t + 1) * P)
+                nc.tensor.matmul_mx(out=acc[:, at : at + c1 - c0], lhsT=w_codes[:, rows].bitcast(FP8X4), lhsT_scale=w_sc[:, rows],
+                                    rhs=x_codes[:, c0:c1].bitcast(FP8X4), rhs_scale=x_sc[:, c0:c1],
+                                    start=True, stop=True)
+                at = at + c1 - c0
+            copy(out=out, in_=acc[:])
 
-        def values(t, c0, c1, copy):
-            acc = psum.tile([P, c1 - c0], F32, name="acc%d_%d" % (t, c0))
-            rows = slice(t * P, (t + 1) * P)
-            nc.tensor.matmul_mx(out=acc[:], lhsT=w_codes[:, rows].bitcast(FP8X4), lhsT_scale=w_sc[:, rows],
-                                rhs=x_codes[:, c0:c1].bitcast(FP8X4), rhs_scale=x_sc[:, c0:c1],
-                                start=True, stop=True)
-            copy(out=y[t][:, c0:c1], in_=acc[:])
+        def placed(t, c0, c1):
+            return window[t][:].indirect(offsets[:, c0 // LIST : c1 // LIST])
 
-        def scatter(t, c0, c1):
-            target = window[t][:].indirect(offsets[:, c0 // LIST : c1 // LIST])
-            if t % 2:
-                nc.vector.tensor_copy(target, y[t][:, c0:c1])
-            else:
-                nc.scalar.activation(target, y[t][:, c0:c1], COPY)
+        def scatter_on_vector(t, c0, c1, source):
+            nc.vector.tensor_copy(placed(t, c0, c1), source)
+
+        def scatter_on_scalar(t, c0, c1, source):
+            nc.scalar.activation(placed(t, c0, c1), source, COPY)
 
         def round_on_gpsimd(out, in_):
             nc.gpsimd.tensor_scalar(out=out, in0=in_, scalar1=1.0, scalar2=-0.0, op0=mybir.AluOpType.mult, op1=mybir.AluOpType.add)
 
-        sides = ((0, SPLIT), (SPLIT, U))
-        pairs = [keep.tile([P, (c1 - c0) * PACK], BF16, name="pairs%d" % c0) for c0, c1 in sides]
+        shared = keep.tile([P, 2 * (U + T)], F32, name="shared")
         lined = {c0: keep.tile([P, (c1 - c0) * PACK], BF16, name="lined%d" % c0, align_bytes=64) for c0, c1 in ON_VECTOR + ON_SCALAR}
 
         def pairs_of(view, c0, c1):
-            side = int(c0 >= SPLIT)
-            base = sides[side][0]
-            return view(pairs[side][:])[:, :, c0 - base : c1 - base]
+            return view(shared[:].bitcast(BF16))[:, :, c0:c1]
 
         def round_place(copy, t, c0, c1):
             places = pairs_of(lambda ap: ap.rearrange("p (u c e) -> p u c e", u=2, e=2), c0, c1)
@@ -105,23 +102,30 @@ def tile_picked_wkvput_none_lo_kernel(tc, x_words, x_scales, mem, w1, slot, out_
             words = pairs_of(lambda ap: ap.bitcast(kind).rearrange("p (u c) -> p u c", u=2), c0, c1)
             copy(out=lined[c0][:].bitcast(kind).rearrange("p (c u) -> p c u", u=2), in_=words.rearrange("p u c -> p c u"))
 
-        values(0, 0, HALF, nc.vector.tensor_copy)
-        scatter(0, 0, HALF)
-        values(1, 0, HALF, nc.vector.tensor_copy)
-        values(1, HALF, T, nc.vector.tensor_copy)
-        values(0, HALF, T, nc.vector.tensor_copy)
-        values(2, 0, HALF, nc.scalar.copy)
-        values(2, HALF, T, nc.scalar.copy)
-        scatter(0, HALF, T)
-        scatter(1, 0, T)
+        y0c = shared[:, U - HALF : U]
+        y2a = shared[:, U : U + HALF]
+        y3 = shared[:, U + HALF : U + HALF + T]
+        y0a = shared[:, U + HALF - P // 2 : U + HALF + P // 2]
+        y0b = keep.tile([P, P], F32, name="y0b")
+        y1 = keep.tile([P, T], F32, name="y1")
+        y2b = keep.tile([P, HALF], F32, name="y2b")
+        values("acc0a", ((0, 0, P),), nc.vector.tensor_copy, y0a)
+        scatter_on_scalar(0, 0, P, y0a)
+        values("acc0b", ((0, P, HALF),), nc.vector.tensor_copy, y0b[:])
+        values("acc1a", ((1, 0, HALF),), nc.vector.tensor_copy, y1[:, :HALF])
+        values("acc1b", ((1, HALF, T),), nc.vector.tensor_copy, y1[:, HALF:])
+        values("acc2b", ((2, HALF, T),), nc.vector.tensor_copy, y2b[:])
+        scatter_on_vector(0, P, HALF, y0b[:])
+        values("acc0c", ((0, HALF, T), (2, 0, HALF)), nc.scalar.copy, shared[:, U - HALF : U + HALF])
+        values("acc3", ((3, 0, T),), nc.scalar.copy, y3)
+        scatter_on_scalar(0, HALF, T, y0c)
+        scatter_on_vector(1, 0, T, y1[:])
         for t in range(2):
             nc.sync.dma_start(out=rows_of(out_0, t), in_=window[t][:])
-            for c0, c1 in sides:
-                round_place(round_on_gpsimd, t, c0, c1)
-        values(3, 0, T, nc.vector.tensor_copy)
-        scatter(3, 0, T)
-        scatter(2, 0, HALF)
-        scatter(2, HALF, T)
+            round_place(round_on_gpsimd, t, 0, U)
+        scatter_on_scalar(2, 0, HALF, y2a)
+        scatter_on_scalar(2, HALF, T, y2b[:])
+        scatter_on_vector(3, 0, T, y3)
         for t in (2, 3):
             nc.sync.dma_start(out=rows_of(out_0, t), in_=window[t][:])
         round_place(nc.scalar.copy, 2, SPLIT, U)

@@ -19,6 +19,7 @@ PACK = 4
 LIST = 16
 HALF = 256
 SPLIT = 512
+TAKEN = 192
 ON_VECTOR = ((0, 256), (256, SPLIT))
 ON_SCALAR = ((SPLIT, 768), (768, 896), (896, 1024))
 STORED = (512, 768, 1024)
@@ -102,30 +103,24 @@ def tile_picked_wkvput_none_lo_kernel(tc, x_words, x_scales, mem, w1, slot, out_
             words = pairs_of(lambda ap: ap.bitcast(kind).rearrange("p (u c) -> p u c", u=2), c0, c1)
             copy(out=lined[c0][:].bitcast(kind).rearrange("p (c u) -> p c u", u=2), in_=words.rearrange("p u c -> p c u"))
 
-        y0c = shared[:, U - HALF : U]
-        y2a = shared[:, U : U + HALF]
-        y3 = shared[:, U + HALF : U + HALF + T]
-        y0a = shared[:, U + HALF - P // 2 : U + HALF + P // 2]
-        y0b = keep.tile([P, P], F32, name="y0b")
-        y1 = keep.tile([P, T], F32, name="y1")
-        y2b = keep.tile([P, HALF], F32, name="y2b")
-        values("acc0a", ((0, 0, P),), nc.vector.tensor_copy, y0a)
-        scatter_on_scalar(0, 0, P, y0a)
-        values("acc0b", ((0, P, HALF),), nc.vector.tensor_copy, y0b[:])
-        values("acc1a", ((1, 0, HALF),), nc.vector.tensor_copy, y1[:, :HALF])
-        values("acc1b", ((1, HALF, T),), nc.vector.tensor_copy, y1[:, HALF:])
-        values("acc2b", ((2, HALF, T),), nc.vector.tensor_copy, y2b[:])
-        scatter_on_vector(0, P, HALF, y0b[:])
-        values("acc0c", ((0, HALF, T), (2, 0, HALF)), nc.scalar.copy, shared[:, U - HALF : U + HALF])
-        values("acc3", ((3, 0, T),), nc.scalar.copy, y3)
-        scatter_on_scalar(0, HALF, T, y0c)
-        scatter_on_vector(1, 0, T, y1[:])
+        held = [keep.tile([P, T], F32, name="y%d" % t) for t in range(3)]
+        y = [tile[:] for tile in held] + [shared[:, U + HALF : U + HALF + T]]
+        values("acc0a", ((0, 0, P),), nc.scalar.copy, y[0][:, :P])
+        scatter_on_vector(0, 0, P, y[0][:, :P])
+        values("acc0b", ((0, P, HALF), (0, HALF, T)), nc.scalar.copy, y[0][:, P:])
+        scatter_on_vector(0, P, T, y[0][:, P:])
+        for t in (1, 2):
+            values("acc%d" % t, ((t, 0, T),), nc.scalar.copy, y[t])
+        for c0, c1 in ((0, HALF), (HALF, T - P), (T - P, T)):
+            values("acc3_%d" % c0, ((3, c0, c1),), nc.scalar.copy, y[3][:, c0:c1])
+        scatter_on_scalar(1, 0, HALF, y[1][:, :HALF])
+        scatter_on_scalar(1, HALF, T, y[1][:, HALF:])
         for t in range(2):
             nc.sync.dma_start(out=rows_of(out_0, t), in_=window[t][:])
             round_place(round_on_gpsimd, t, 0, U)
-        scatter_on_scalar(2, 0, HALF, y2a)
-        scatter_on_scalar(2, HALF, T, y2b[:])
-        scatter_on_vector(3, 0, T, y3)
+        scatter_on_vector(2, 0, TAKEN, y[2][:, :TAKEN])
+        scatter_on_scalar(2, TAKEN, T, y[2][:, TAKEN:])
+        scatter_on_vector(3, 0, T, y[3])
         for t in (2, 3):
             nc.sync.dma_start(out=rows_of(out_0, t), in_=window[t][:])
         round_place(nc.scalar.copy, 2, SPLIT, U)

@@ -20,6 +20,7 @@ LIST = 16
 HALF = 256
 SPLIT = 512
 TAKEN = 192
+W_CUTS = ((0, 384), (384, 512))
 ON_VECTOR = ((0, 256), (256, SPLIT))
 ON_SCALAR = ((SPLIT, 768), (768, 896), (896, 1024))
 STORED = (512, 768, 1024)
@@ -34,7 +35,7 @@ def tile_picked_wkvput_none_lo_kernel(tc, x_words, x_scales, mem, w1, slot, out_
         offsets = keep.tile([P, T // LIST], U16, name="offsets")
         x_sc = keep.tile([P, T], U8, name="x_sc", align_bytes=64)
         x_codes = keep.tile([P, T], I32, name="x_codes", align_bytes=64)
-        w_raw = [keep.tile([P, PACK, N // 2], F32, name="w_raw%d" % h) for h in range(2)]
+        w_raw = [keep.tile([P, PACK, c1 - c0], F32, name="w_raw%d" % c0) for c0, c1 in W_CUTS]
         window = [keep.tile([P, U], F32, name="window%d" % t) for t in range(PACK)]
         nc.gpsimd.memset(x_sc[:].bitcast(I32), 0)
 
@@ -44,23 +45,24 @@ def tile_picked_wkvput_none_lo_kernel(tc, x_words, x_scales, mem, w1, slot, out_
         sc_rows = x_scales[0].bitcast(I32)
         w_rows = w1.rearrange("(p j) c -> p j c", j=PACK)
         x_cols = x_words[0].rearrange("p c r -> p (c r)").bitcast(I32)
-        nc.sync.dma_start(offsets[:], slot)
-        nc.sync.dma_start(out=w_raw[0][:], in_=w_rows[:, :, : N // 2])
-        nc.sync.dma_start(out=w_raw[1][:], in_=w_rows[:, :, N // 2 :])
+        for raw, (c0, c1) in zip(w_raw, W_CUTS):
+            nc.sync.dma_start(out=raw[:], in_=w_rows[:, :, c0:c1])
         for r in range(4):
             queue = nc.sync if r % 2 else nc.scalar
             queue.dma_start(out=x_sc[r:P:32, :].bitcast(I32), in_=sc_rows[r:16:4, :])
         nc.sync.dma_start(out=x_codes[:], in_=x_cols)
-        for t in range(PACK):
+        nc.sync.dma_start(out=window[0][:], in_=rows_of(mem, 0))
+        nc.sync.dma_start(offsets[:], slot)
+        for t in range(1, PACK):
             nc.sync.dma_start(out=window[t][:], in_=rows_of(mem, t))
 
         w_codes = keep.tile([P, N], I32, name="w_codes", align_bytes=64)
         w_sc = keep.tile([P, N], U8, name="w_sc", align_bytes=64)
         grouped = [keep.tile([P, 2, P, PACK], BF16, name="grouped%d" % u, align_bytes=64) for u in range(2)]
-        for h in range(2):
-            src = w_raw[h][:].rearrange("p j (l t) -> p l j t", t=PACK)
+        for raw, (c0, c1) in zip(w_raw, W_CUTS):
+            src = raw[:].rearrange("p j (l t) -> p l j t", t=PACK)
             for u, copy in enumerate((nc.vector.tensor_copy, nc.scalar.copy)):
-                dst = grouped[u][:, :, h * P // 2 : (h + 1) * P // 2, :].rearrange("p e l j -> p l j e")
+                dst = grouped[u][:, :, c0 // PACK : c1 // PACK, :].rearrange("p e l j -> p l j e")
                 copy(out=dst, in_=src[:, :, :, 2 * u : 2 * u + 2])
         for t in range(PACK):
             nc.vector.quantize_mx(out=w_codes[:, t * P : (t + 1) * P].bitcast(FP8X4), scales=w_sc[:, t * P : (t + 1) * P],

@@ -107,21 +107,20 @@ def tile_picked_wkvput_none_lo_kernel(tc, x_words, x_scales, mem, w1, slot, out_
 
         held = [keep.tile([P, T], F32, name="y%d" % t) for t in range(3)]
         y = [tile[:] for tile in held] + [shared[:, U + HALF : U + HALF + T]]
-        values("acc0a", ((0, 0, P),), nc.scalar.copy, y[0][:, :P])
-        scatter_on_vector(0, 0, P, y[0][:, :P])
-        values("acc0b", ((0, P, HALF), (0, HALF, T)), nc.scalar.copy, y[0][:, P:])
-        scatter_on_vector(0, P, T, y[0][:, P:])
-        for t in (1, 2):
-            values("acc%d" % t, ((t, 0, T),), nc.scalar.copy, y[t])
+        values("acc0a", ((0, 0, P), (0, P, TAKEN)), nc.scalar.copy, y[0][:, :TAKEN])
+        scatter_on_vector(0, 0, TAKEN, y[0][:, :TAKEN])
+        values("acc1", ((1, 0, T),), nc.scalar.copy, y[1])
+        scatter_on_vector(1, 0, T, y[1])
+        values("acc0b", ((0, TAKEN, HALF), (0, HALF, T)), nc.scalar.copy, y[0][:, TAKEN:])
+        values("acc2", ((2, 0, T),), nc.scalar.copy, y[2])
         for c0, c1 in ((0, HALF), (HALF, T - P), (T - P, T)):
             values("acc3_%d" % c0, ((3, c0, c1),), nc.scalar.copy, y[3][:, c0:c1])
-        scatter_on_scalar(1, 0, HALF, y[1][:, :HALF])
-        scatter_on_scalar(1, HALF, T, y[1][:, HALF:])
+        scatter_on_scalar(0, TAKEN, T, y[0][:, TAKEN:])
         for t in range(2):
             nc.sync.dma_start(out=rows_of(out_0, t), in_=window[t][:])
             round_place(round_on_gpsimd, t, 0, U)
-        scatter_on_vector(2, 0, TAKEN, y[2][:, :TAKEN])
-        scatter_on_scalar(2, TAKEN, T, y[2][:, TAKEN:])
+        scatter_on_scalar(2, 0, HALF, y[2][:, :HALF])
+        scatter_on_scalar(2, HALF, T, y[2][:, HALF:])
         scatter_on_vector(3, 0, T, y[3])
         for t in (2, 3):
             nc.sync.dma_start(out=rows_of(out_0, t), in_=window[t][:])

@@ -18,12 +18,13 @@ P = 128
 PACK = 4
 LIST = 16
 HALF = 256
-SPLIT = 512
-TAKEN = 192
+SPLIT = 640
+TAKEN = 128
 W_CUTS = ((0, 384), (384, 512))
 ON_VECTOR = ((0, 256), (256, SPLIT))
-ON_SCALAR = ((SPLIT, 768), (768, 896), (896, 1024))
-STORED = (512, 768, 1024)
+ON_SCALAR = ((SPLIT, 896), (896, 1024))
+QUANTISED = ((0, 256), (256, 512), (512, SPLIT), (SPLIT, 896), (896, 1024))
+STORED = (512, 896, 1024)
 
 
 def tile_picked_wkvput_none_lo_kernel(tc, x_words, x_scales, mem, w1, slot, out_0, out_1, out_2):
@@ -59,11 +60,18 @@ def tile_picked_wkvput_none_lo_kernel(tc, x_words, x_scales, mem, w1, slot, out_
         w_codes = keep.tile([P, N], I32, name="w_codes", align_bytes=64)
         w_sc = keep.tile([P, N], U8, name="w_sc", align_bytes=64)
         grouped = [keep.tile([P, 2, P, PACK], BF16, name="grouped%d" % u, align_bytes=64) for u in range(2)]
-        for raw, (c0, c1) in zip(w_raw, W_CUTS):
-            src = raw[:].rearrange("p j (l t) -> p l j t", t=PACK)
-            for u, copy in enumerate((nc.vector.tensor_copy, nc.scalar.copy)):
-                dst = grouped[u][:, :, c0 // PACK : c1 // PACK, :].rearrange("p e l j -> p l j e")
-                copy(out=dst, in_=src[:, :, :, 2 * u : 2 * u + 2])
+
+        def deal(copy, load, u, l0, l1):
+            at = W_CUTS[load][0] // PACK
+            src = w_raw[load][:].rearrange("p j (l t) -> p l j t", t=PACK)[:, l0 - at : l1 - at, :, 2 * u : 2 * u + 2]
+            copy(out=grouped[u][:, :, l0:l1, :].rearrange("p e l j -> p l j e"), in_=src)
+
+        early = W_CUTS[0][1] // PACK
+        deal(nc.vector.tensor_copy, 0, 0, 0, early)
+        deal(nc.scalar.copy, 0, 1, 0, early // 2)
+        deal(nc.vector.tensor_copy, 0, 1, early // 2, early)
+        for u in range(2):
+            deal(nc.scalar.copy, 1, u, early, P)
         for t in range(PACK):
             nc.vector.quantize_mx(out=w_codes[:, t * P : (t + 1) * P].bitcast(FP8X4), scales=w_sc[:, t * P : (t + 1) * P],
                                   in_=grouped[t // 2][:, t % 2].rearrange("p l j -> p (l j)"))
@@ -91,41 +99,39 @@ def tile_picked_wkvput_none_lo_kernel(tc, x_words, x_scales, mem, w1, slot, out_
         def round_on_gpsimd(out, in_):
             nc.gpsimd.tensor_scalar(out=out, in0=in_, scalar1=1.0, scalar2=-0.0, op0=mybir.AluOpType.mult, op1=mybir.AluOpType.add)
 
-        shared = keep.tile([P, 2 * (U + T)], F32, name="shared")
-        lined = {c0: keep.tile([P, (c1 - c0) * PACK], BF16, name="lined%d" % c0, align_bytes=64) for c0, c1 in ON_VECTOR + ON_SCALAR}
-
-        def pairs_of(view, c0, c1):
-            return view(shared[:].bitcast(BF16))[:, :, c0:c1]
+        pairs = keep.tile([P, 2 * U], F32, name="pairs")
+        lined = keep.tile([P, U * PACK], BF16, name="lined", align_bytes=64)
 
         def round_place(copy, t, c0, c1):
-            places = pairs_of(lambda ap: ap.rearrange("p (u c e) -> p u c e", u=2, e=2), c0, c1)
-            copy(out=places[:, t // 2, :, t % 2], in_=window[t][:, c0:c1])
+            places = pairs[:].bitcast(BF16).rearrange("p (u c e) -> p u c e", u=2, e=2)
+            copy(out=places[:, t // 2, c0:c1, t % 2], in_=window[t][:, c0:c1])
 
         def line_up(copy, kind, c0, c1):
-            words = pairs_of(lambda ap: ap.bitcast(kind).rearrange("p (u c) -> p u c", u=2), c0, c1)
-            copy(out=lined[c0][:].bitcast(kind).rearrange("p (c u) -> p c u", u=2), in_=words.rearrange("p u c -> p c u"))
+            words = pairs[:].bitcast(kind).rearrange("p (u c) -> p u c", u=2)[:, :, c0:c1]
+            copy(out=lined[:].bitcast(kind).rearrange("p (c u) -> p c u", u=2)[:, c0:c1], in_=words.rearrange("p u c -> p c u"))
 
-        held = [keep.tile([P, T], F32, name="y%d" % t) for t in range(3)]
-        y = [tile[:] for tile in held] + [shared[:, U + HALF : U + HALF + T]]
-        values("acc0a", ((0, 0, P), (0, P, TAKEN)), nc.scalar.copy, y[0][:, :TAKEN])
+        held = {t: keep.tile([P, T], F32, name="y%d" % t) for t in range(2)}
+        y = [held[0][:], held[1][:], pairs[:, U : U + T], pairs[:, U + T :]]
+        values("acc0a", ((0, 0, TAKEN),), nc.scalar.copy, y[0][:, :TAKEN])
         scatter_on_vector(0, 0, TAKEN, y[0][:, :TAKEN])
-        values("acc1", ((1, 0, T),), nc.scalar.copy, y[1])
+        for c0, c1 in ((0, HALF), (HALF, T)):
+            values("acc1_%d" % c0, ((1, c0, c1),), nc.scalar.copy, y[1][:, c0:c1])
         scatter_on_vector(1, 0, T, y[1])
         values("acc0b", ((0, TAKEN, HALF), (0, HALF, T)), nc.scalar.copy, y[0][:, TAKEN:])
         values("acc2", ((2, 0, T),), nc.scalar.copy, y[2])
-        for c0, c1 in ((0, HALF), (HALF, T - P), (T - P, T)):
-            values("acc3_%d" % c0, ((3, c0, c1),), nc.scalar.copy, y[3][:, c0:c1])
+        values("acc3a", ((3, 0, HALF), (3, HALF, T - P)), nc.scalar.copy, y[3][:, : T - P])
+        values("acc3b", ((3, T - P, T),), nc.scalar.copy, y[3][:, T - P :])
         scatter_on_scalar(0, TAKEN, T, y[0][:, TAKEN:])
         for t in range(2):
             nc.sync.dma_start(out=rows_of(out_0, t), in_=window[t][:])
             round_place(round_on_gpsimd, t, 0, U)
-        scatter_on_scalar(2, 0, HALF, y[2][:, :HALF])
-        scatter_on_scalar(2, HALF, T, y[2][:, HALF:])
-        scatter_on_vector(3, 0, T, y[3])
+        scatter_on_vector(2, 0, T, y[2])
+        scatter_on_scalar(3, 0, HALF, y[3][:, :HALF])
+        scatter_on_scalar(3, HALF, T, y[3][:, HALF:])
         for t in (2, 3):
             nc.sync.dma_start(out=rows_of(out_0, t), in_=window[t][:])
-        round_place(nc.scalar.copy, 2, SPLIT, U)
         round_place(nc.vector.tensor_copy, 2, 0, SPLIT)
+        round_place(nc.scalar.copy, 2, SPLIT, U)
         for c0, c1 in ON_VECTOR:
             round_place(nc.vector.tensor_copy, 3, c0, c1)
         for c0, c1 in ON_VECTOR:
@@ -139,8 +145,8 @@ def tile_picked_wkvput_none_lo_kernel(tc, x_words, x_scales, mem, w1, slot, out_
         o_codes = keep.tile([P, U], I32, name="o_codes", align_bytes=64)
         o_words = out_1[0].rearrange("p c r -> p (c r)").bitcast(I32)
         stored = 0
-        for c0, c1 in ON_VECTOR + ON_SCALAR:
-            nc.vector.quantize_mx(out=o_codes[:, c0:c1].bitcast(FP8X4), scales=o_sc[:, c0:c1], in_=lined[c0][:])
+        for c0, c1 in QUANTISED:
+            nc.vector.quantize_mx(out=o_codes[:, c0:c1].bitcast(FP8X4), scales=o_sc[:, c0:c1], in_=lined[:, c0 * PACK : c1 * PACK])
             if c1 in STORED:
                 nc.sync.dma_start(out=o_words[:, stored:c1], in_=o_codes[:, stored:c1])
                 stored = c1

@@ -110,24 +110,29 @@ def tile_picked_wkvput_none_lo_kernel(tc, x_words, x_scales, mem, w1, slot, out_
             words = pairs[:].bitcast(kind).rearrange("p (u c) -> p u c", u=2)[:, :, c0:c1]
             copy(out=lined[:].bitcast(kind).rearrange("p (c u) -> p c u", u=2)[:, c0:c1], in_=words.rearrange("p u c -> p c u"))
 
-        held = {t: keep.tile([P, T], F32, name="y%d" % t) for t in range(2)}
-        y = [held[0][:], held[1][:], pairs[:, U : U + T], pairs[:, U + T :]]
-        values("acc0a", ((0, 0, TAKEN),), nc.scalar.copy, y[0][:, :TAKEN])
-        scatter_on_vector(0, 0, TAKEN, y[0][:, :TAKEN])
+        high = pairs[:, U:]
+        first = high[:, SPLIT - TAKEN // 2 : SPLIT + TAKEN // 2]
+        rest = keep.tile([P, T - TAKEN], F32, name="rest")
+        y1 = keep.tile([P, T], F32, name="y1")
+        y2 = high[:, SPLIT - T : SPLIT]
+        y3_early = keep.tile([P, HALF], F32, name="y3_early")
+        y3_late = high[:, SPLIT : SPLIT + HALF]
+        values("acc0a", ((0, 0, TAKEN),), nc.scalar.copy, first)
+        scatter_on_vector(0, 0, TAKEN, first)
+        values("acc0b", ((0, TAKEN, HALF), (0, HALF, T)), nc.scalar.copy, rest[:])
         for c0, c1 in ((0, HALF), (HALF, T)):
-            values("acc1_%d" % c0, ((1, c0, c1),), nc.scalar.copy, y[1][:, c0:c1])
-        scatter_on_vector(1, 0, T, y[1])
-        values("acc0b", ((0, TAKEN, HALF), (0, HALF, T)), nc.scalar.copy, y[0][:, TAKEN:])
-        values("acc2", ((2, 0, T),), nc.scalar.copy, y[2])
-        values("acc3a", ((3, 0, HALF), (3, HALF, T - P)), nc.scalar.copy, y[3][:, : T - P])
-        values("acc3b", ((3, T - P, T),), nc.scalar.copy, y[3][:, T - P :])
-        scatter_on_scalar(0, TAKEN, T, y[0][:, TAKEN:])
+            values("acc1_%d" % c0, ((1, c0, c1),), nc.scalar.copy, y1[:, c0:c1])
+        scatter_on_vector(1, 0, T, y1[:])
+        values("acc3b", ((3, HALF, T),), nc.scalar.copy, y3_early[:])
+        scatter_on_scalar(0, TAKEN, T, rest[:])
+        values("acc2", ((2, 0, T),), nc.scalar.copy, y2)
+        values("acc3a", ((3, 0, HALF),), nc.scalar.copy, y3_late)
         for t in range(2):
             nc.sync.dma_start(out=rows_of(out_0, t), in_=window[t][:])
             round_place(round_on_gpsimd, t, 0, U)
-        scatter_on_vector(2, 0, T, y[2])
-        scatter_on_scalar(3, 0, HALF, y[3][:, :HALF])
-        scatter_on_scalar(3, HALF, T, y[3][:, HALF:])
+        scatter_on_vector(2, 0, T, y2)
+        scatter_on_scalar(3, HALF, T, y3_early[:])
+        scatter_on_scalar(3, 0, HALF, y3_late)
         for t in (2, 3):
             nc.sync.dma_start(out=rows_of(out_0, t), in_=window[t][:])
         round_place(nc.vector.tensor_copy, 2, 0, SPLIT)

@@ -18,12 +18,13 @@ P = 128
 PACK = 4
 LIST = 16
 HALF = 256
-SPLIT = 640
+SPLIT = 576
 TAKEN = 128
 W_CUTS = ((0, 384), (384, 512))
 ON_VECTOR = ((0, 256), (256, SPLIT))
-ON_SCALAR = ((SPLIT, 896), (896, 1024))
-QUANTISED = ((0, 256), (256, 512), (512, SPLIT), (SPLIT, 896), (896, 1024))
+ROUNDED_ON_SCALAR = ((SPLIT, 768), (768, 1024))
+LINED_ON_SCALAR = ((SPLIT, 768), (768, 896), (896, 1024))
+QUANTISED = ((0, 256), (256, 512), (512, 768), (768, 896), (896, 1024))
 STORED = (512, 896, 1024)
 
 
@@ -141,9 +142,9 @@ def tile_picked_wkvput_none_lo_kernel(tc, x_words, x_scales, mem, w1, slot, out_
             round_place(nc.vector.tensor_copy, 3, c0, c1)
         for c0, c1 in ON_VECTOR:
             line_up(nc.vector.tensor_copy, I32, c0, c1)
-        for c0, c1 in ON_SCALAR:
+        for c0, c1 in ROUNDED_ON_SCALAR:
             round_place(nc.scalar.copy, 3, c0, c1)
-        for c0, c1 in ON_SCALAR:
+        for c0, c1 in LINED_ON_SCALAR:
             line_up(nc.scalar.copy, U32, c0, c1)
 
         o_sc = keep.tile([P, U], U8, name="o_sc", align_bytes=64)

@@ -17,6 +17,7 @@ COPY = mybir.ActivationFunctionType.Copy
 P = 128
 PACK = 4
 LIST = 16
+X_ROW = 4
 HALF = 256
 SPLIT = 576
 TAKEN = 128
@@ -35,11 +36,10 @@ def tile_picked_wkvput_none_lo_kernel(tc, x_words, x_scales, mem, w1, slot, out_
         psum = ctx.enter_context(tc.psum_pool(name="psum", bufs=1))
 
         offsets = keep.tile([P, T // LIST], U16, name="offsets")
-        x_sc = keep.tile([P, T], U8, name="x_sc", align_bytes=64)
+        planes = keep.tile([P, T], U8, name="planes", align_bytes=64)
         x_codes = keep.tile([P, T], I32, name="x_codes", align_bytes=64)
         w_raw = [keep.tile([P, PACK, c1 - c0], F32, name="w_raw%d" % c0) for c0, c1 in W_CUTS]
         window = [keep.tile([P, U], F32, name="window%d" % t) for t in range(PACK)]
-        nc.gpsimd.memset(x_sc[:].bitcast(I32), 0)
 
         def rows_of(dram, t):
             return dram.rearrange("(l t) c -> l t c", t=PACK)[:, t, :]
@@ -47,11 +47,15 @@ def tile_picked_wkvput_none_lo_kernel(tc, x_words, x_scales, mem, w1, slot, out_
         sc_rows = x_scales[0].bitcast(I32)
         w_rows = w1.rearrange("(p j) c -> p j c", j=PACK)
         x_cols = x_words[0].rearrange("p c r -> p (c r)").bitcast(I32)
-        for raw, (c0, c1) in zip(w_raw, W_CUTS):
-            nc.sync.dma_start(out=raw[:], in_=w_rows[:, :, c0:c1])
-        for r in range(4):
-            queue = nc.sync if r % 2 else nc.scalar
-            queue.dma_start(out=x_sc[r:P:32, :].bitcast(I32), in_=sc_rows[r:16:4, :])
+
+        def load_scale_row(queue, r):
+            queue.dma_start(out=planes[X_ROW + r : P : 32, :].bitcast(I32), in_=sc_rows[r:16:4, :])
+
+        for r, (c0, c1) in enumerate(W_CUTS):
+            nc.sync.dma_start(out=w_raw[r][:], in_=w_rows[:, :, c0:c1])
+            load_scale_row(nc.scalar, r)
+        for r in (2, 3):
+            load_scale_row(nc.sync, r)
         nc.sync.dma_start(out=x_codes[:], in_=x_cols)
         nc.sync.dma_start(out=window[0][:], in_=rows_of(mem, 0))
         nc.sync.dma_start(offsets[:], slot)
@@ -59,7 +63,6 @@ def tile_picked_wkvput_none_lo_kernel(tc, x_words, x_scales, mem, w1, slot, out_
             nc.sync.dma_start(out=window[t][:], in_=rows_of(mem, t))
 
         w_codes = keep.tile([P, N], I32, name="w_codes", align_bytes=64)
-        w_sc = keep.tile([P, N], U8, name="w_sc", align_bytes=64)
         grouped = [keep.tile([P, 2, P, PACK], BF16, name="grouped%d" % u, align_bytes=64) for u in range(2)]
 
         def deal(copy, load, u, l0, l1):
@@ -73,17 +76,18 @@ def tile_picked_wkvput_none_lo_kernel(tc, x_words, x_scales, mem, w1, slot, out_
         deal(nc.vector.tensor_copy, 0, 1, early // 2, early)
         for u in range(2):
             deal(nc.scalar.copy, 1, u, early, P)
-        for t in range(PACK):
-            nc.vector.quantize_mx(out=w_codes[:, t * P : (t + 1) * P].bitcast(FP8X4), scales=w_sc[:, t * P : (t + 1) * P],
-                                  in_=grouped[t // 2][:, t % 2].rearrange("p l j -> p (l j)"))
+        for t, l0, l1 in [(0, 0, P // 2), (0, P // 2, P)] + [(t, 0, P) for t in range(1, PACK)]:
+            cols = slice(t * P + l0, t * P + l1)
+            nc.vector.quantize_mx(out=w_codes[:, cols].bitcast(FP8X4), scales=planes[:, cols],
+                                  in_=grouped[t // 2][:, t % 2, l0:l1].rearrange("p l j -> p (l j)"))
 
         def values(name, pieces, copy, out):
             acc = psum.tile([P, sum(c1 - c0 for t, c0, c1 in pieces)], F32, name=name)
             at = 0
             for t, c0, c1 in pieces:
                 rows = slice(t * P, (t + 1) * P)
-                nc.tensor.matmul_mx(out=acc[:, at : at + c1 - c0], lhsT=w_codes[:, rows].bitcast(FP8X4), lhsT_scale=w_sc[:, rows],
-                                    rhs=x_codes[:, c0:c1].bitcast(FP8X4), rhs_scale=x_sc[:, c0:c1],
+                nc.tensor.matmul_mx(out=acc[:, at : at + c1 - c0], lhsT=w_codes[:, rows].bitcast(FP8X4), lhsT_scale=planes[:, rows],
+                                    rhs=x_codes[:, c0:c1].bitcast(FP8X4), rhs_scale=planes[X_ROW:, c0:c1],
                                     start=True, stop=True)
                 at = at + c1 - c0
             copy(out=out, in_=acc[:])

@@ -20,7 +20,7 @@ LIST = 16
 X_ROW = 4
 HALF = 256
 SPLIT = 576
-TAKEN = 128
+TAKEN = 160
 W_CUTS = ((0, 384), (384, 512))
 ON_VECTOR = ((0, 256), (256, SPLIT))
 ROUNDED_ON_SCALAR = ((SPLIT, 768), (768, 1024))
@@ -59,7 +59,7 @@ def tile_picked_wkvput_none_lo_kernel(tc, x_words, x_scales, mem, w1, slot, out_
         nc.sync.dma_start(out=x_codes[:], in_=x_cols)
         nc.sync.dma_start(out=window[0][:], in_=rows_of(mem, 0))
         nc.sync.dma_start(offsets[:], slot)
-        for t in range(1, PACK):
+        for t in (1, 3, 2):
             nc.sync.dma_start(out=window[t][:], in_=rows_of(mem, t))
 
         w_codes = keep.tile([P, N], I32, name="w_codes", align_bytes=64)
@@ -115,39 +115,40 @@ def tile_picked_wkvput_none_lo_kernel(tc, x_words, x_scales, mem, w1, slot, out_
             words = pairs[:].bitcast(kind).rearrange("p (u c) -> p u c", u=2)[:, :, c0:c1]
             copy(out=lined[:].bitcast(kind).rearrange("p (c u) -> p c u", u=2)[:, c0:c1], in_=words.rearrange("p u c -> p c u"))
 
-        high = pairs[:, U:]
-        first = high[:, SPLIT - TAKEN // 2 : SPLIT + TAKEN // 2]
-        rest = keep.tile([P, T - TAKEN], F32, name="rest")
-        y1 = keep.tile([P, T], F32, name="y1")
-        y2 = high[:, SPLIT - T : SPLIT]
-        y3_early = keep.tile([P, HALF], F32, name="y3_early")
-        y3_late = high[:, SPLIT : SPLIT + HALF]
-        values("acc0a", ((0, 0, TAKEN),), nc.scalar.copy, first)
-        scatter_on_vector(0, 0, TAKEN, first)
-        values("acc0b", ((0, TAKEN, HALF), (0, HALF, T)), nc.scalar.copy, rest[:])
-        for c0, c1 in ((0, HALF), (HALF, T)):
-            values("acc1_%d" % c0, ((1, c0, c1),), nc.scalar.copy, y1[:, c0:c1])
-        scatter_on_vector(1, 0, T, y1[:])
-        values("acc3b", ((3, HALF, T),), nc.scalar.copy, y3_early[:])
-        scatter_on_scalar(0, TAKEN, T, rest[:])
-        values("acc2", ((2, 0, T),), nc.scalar.copy, y2)
-        values("acc3a", ((3, 0, HALF),), nc.scalar.copy, y3_late)
+        held = [keep.tile([P, T], F32, name="y%d" % t) for t in range(2)]
+        y = [held[0][:], held[1][:], pairs[:, U : U + T], pairs[:, U + T :]]
+
+        def half(t, h):
+            values("acc%d_%d" % (t, h), ((t, h * HALF, (h + 1) * HALF),), nc.scalar.copy, y[t][:, h * HALF : (h + 1) * HALF])
+
+        for c0 in (0, P):
+            values("first%d" % c0, ((0, c0, c0 + P),), nc.scalar.copy, y[0][:, c0 : c0 + P])
+        scatter_on_vector(0, 0, HALF, y[0][:, :HALF])
+        half(1, 0)
+        scatter_on_vector(1, 0, HALF, y[1][:, :HALF])
+        half(0, 1)
+        values("acc2", ((2, 0, T),), nc.scalar.copy, y[2])
+        half(3, 0)
+        half(1, 1)
+        half(3, 1)
+        scatter_on_scalar(0, HALF, T, y[0][:, HALF:])
+        scatter_on_scalar(1, HALF, T, y[1][:, HALF:])
         for t in range(2):
             nc.sync.dma_start(out=rows_of(out_0, t), in_=window[t][:])
             round_place(round_on_gpsimd, t, 0, U)
-        scatter_on_vector(2, 0, T, y2)
-        scatter_on_scalar(3, HALF, T, y3_early[:])
-        scatter_on_scalar(3, 0, HALF, y3_late)
-        for t in (2, 3):
+        scatter_on_vector(3, 0, TAKEN, y[3][:, :TAKEN])
+        scatter_on_scalar(3, TAKEN, T, y[3][:, TAKEN:])
+        scatter_on_vector(2, 0, T, y[2])
+        for t in (3, 2):
             nc.sync.dma_start(out=rows_of(out_0, t), in_=window[t][:])
-        round_place(nc.vector.tensor_copy, 2, 0, SPLIT)
-        round_place(nc.scalar.copy, 2, SPLIT, U)
+        round_place(nc.vector.tensor_copy, 3, 0, SPLIT)
         for c0, c1 in ON_VECTOR:
-            round_place(nc.vector.tensor_copy, 3, c0, c1)
+            round_place(nc.vector.tensor_copy, 2, c0, c1)
         for c0, c1 in ON_VECTOR:
             line_up(nc.vector.tensor_copy, I32, c0, c1)
+        round_place(nc.scalar.copy, 3, SPLIT, U)
         for c0, c1 in ROUNDED_ON_SCALAR:
-            round_place(nc.scalar.copy, 3, c0, c1)
+            round_place(nc.scalar.copy, 2, c0, c1)
         for c0, c1 in LINED_ON_SCALAR:
             line_up(nc.scalar.copy, U32, c0, c1)
 

@@ -51,14 +51,16 @@ def tile_picked_wkvput_none_lo_kernel(tc, x_words, x_scales, mem, w1, slot, out_
         def load_scale_row(queue, r):
             queue.dma_start(out=planes[X_ROW + r : P : 32, :].bitcast(I32), in_=sc_rows[r:16:4, :])
 
+        for r in (0, 1):
+            load_scale_row(nc.scalar, r)
         for r, (c0, c1) in enumerate(W_CUTS):
             nc.sync.dma_start(out=w_raw[r][:], in_=w_rows[:, :, c0:c1])
-            load_scale_row(nc.scalar, r)
         for r in (2, 3):
             load_scale_row(nc.sync, r)
-        nc.sync.dma_start(out=x_codes[:], in_=x_cols)
+        nc.sync.dma_start(out=x_codes[:, :HALF], in_=x_cols[:, :HALF])
         nc.sync.dma_start(out=window[0][:], in_=rows_of(mem, 0))
         nc.sync.dma_start(offsets[:], slot)
+        nc.sync.dma_start(out=x_codes[:, HALF:], in_=x_cols[:, HALF:])
         for t in (1, 3, 2):
             nc.sync.dma_start(out=window[t][:], in_=rows_of(mem, t))
 
@@ -74,8 +76,10 @@ def tile_picked_wkvput_none_lo_kernel(tc, x_words, x_scales, mem, w1, slot, out_
         deal(nc.vector.tensor_copy, 0, 0, 0, early)
         deal(nc.scalar.copy, 0, 1, 0, early // 2)
         deal(nc.vector.tensor_copy, 0, 1, early // 2, early)
-        for u in range(2):
-            deal(nc.scalar.copy, 1, u, early, P)
+        late = (early + P) // 2
+        deal(nc.vector.tensor_copy, 1, 0, early, late)
+        deal(nc.scalar.copy, 1, 0, late, P)
+        deal(nc.scalar.copy, 1, 1, early, P)
         for t, l0, l1 in [(0, 0, P // 2), (0, P // 2, P)] + [(t, 0, P) for t in range(1, PACK)]:
             cols = slice(t * P + l0, t * P + l1)
             nc.vector.quantize_mx(out=w_codes[:, cols].bitcast(FP8X4), scales=planes[:, cols],
@@ -126,11 +130,11 @@ def tile_picked_wkvput_none_lo_kernel(tc, x_words, x_scales, mem, w1, slot, out_
         scatter_on_vector(0, 0, HALF, y[0][:, :HALF])
         half(1, 0)
         scatter_on_vector(1, 0, HALF, y[1][:, :HALF])
-        half(0, 1)
-        values("acc2", ((2, 0, T),), nc.scalar.copy, y[2])
         half(3, 0)
-        half(1, 1)
-        half(3, 1)
+        half(2, 0)
+        for t in range(3):
+            half(t, 1)
+        values("first0", ((3, HALF, T),), nc.scalar.copy, y[3][:, HALF:])
         scatter_on_scalar(0, HALF, T, y[0][:, HALF:])
         scatter_on_scalar(1, HALF, T, y[1][:, HALF:])
         for t in range(2):

@@ -22,6 +22,7 @@ HALF = 256
 SPLIT = 576
 TAKEN = 160
 W_CUTS = ((0, 384), (384, 512))
+W_SHARE = 72
 ON_VECTOR = ((0, 256), (256, SPLIT))
 ROUNDED_ON_SCALAR = ((SPLIT, 768), (768, 1024))
 LINED_ON_SCALAR = ((SPLIT, 768), (768, 896), (896, 1024))
@@ -74,8 +75,8 @@ def tile_picked_wkvput_none_lo_kernel(tc, x_words, x_scales, mem, w1, slot, out_
 
         early = W_CUTS[0][1] // PACK
         deal(nc.vector.tensor_copy, 0, 0, 0, early)
-        deal(nc.scalar.copy, 0, 1, 0, early // 2)
-        deal(nc.vector.tensor_copy, 0, 1, early // 2, early)
+        deal(nc.scalar.copy, 0, 1, 0, W_SHARE)
+        deal(nc.vector.tensor_copy, 0, 1, W_SHARE, early)
         late = (early + P) // 2
         deal(nc.vector.tensor_copy, 1, 0, early, late)
         deal(nc.scalar.copy, 1, 0, late, P)

@@ -19,15 +19,16 @@ PACK = 4
 LIST = 16
 X_ROW = 4
 HALF = 256
-SPLIT = 576
-TAKEN = 160
+SPLIT = 544
+FIRST = 224
+TAKEN = 192
 W_CUTS = ((0, 384), (384, 512))
 W_SHARE = 72
 ON_VECTOR = ((0, 256), (256, SPLIT))
 ROUNDED_ON_SCALAR = ((SPLIT, 768), (768, 1024))
 LINED_ON_SCALAR = ((SPLIT, 768), (768, 896), (896, 1024))
-QUANTISED = ((0, 256), (256, 512), (512, 768), (768, 896), (896, 1024))
-STORED = (512, 896, 1024)
+QUANTISED = ((0, 256), (256, 384), (384, 768), (768, 896), (896, 1024))
+STORED = (384, 768, 1024)
 
 
 def tile_picked_wkvput_none_lo_kernel(tc, x_words, x_scales, mem, w1, slot, out_0, out_1, out_2):
@@ -126,17 +127,18 @@ def tile_picked_wkvput_none_lo_kernel(tc, x_words, x_scales, mem, w1, slot, out_
         def half(t, h):
             values("acc%d_%d" % (t, h), ((t, h * HALF, (h + 1) * HALF),), nc.scalar.copy, y[t][:, h * HALF : (h + 1) * HALF])
 
-        for c0 in (0, P):
-            values("first%d" % c0, ((0, c0, c0 + P),), nc.scalar.copy, y[0][:, c0 : c0 + P])
-        scatter_on_vector(0, 0, HALF, y[0][:, :HALF])
+        for c0, copy in ((0, nc.vector.tensor_copy), (P, nc.scalar.copy)):
+            values("first%d" % c0, ((0, c0, c0 + P),), copy, y[0][:, c0 : c0 + P])
+        scatter_on_vector(0, 0, FIRST, y[0][:, :FIRST])
         half(1, 0)
         scatter_on_vector(1, 0, HALF, y[1][:, :HALF])
         half(3, 0)
         half(2, 0)
         for t in range(3):
             half(t, 1)
-        values("first0", ((3, HALF, T),), nc.scalar.copy, y[3][:, HALF:])
-        scatter_on_scalar(0, HALF, T, y[0][:, HALF:])
+        for c0 in (0, P):
+            values("first%d" % c0, ((3, HALF + c0, HALF + c0 + P),), nc.scalar.copy, y[3][:, HALF + c0 : HALF + c0 + P])
+        scatter_on_scalar(0, FIRST, T, y[0][:, FIRST:])
         scatter_on_scalar(1, HALF, T, y[1][:, HALF:])
         for t in range(2):
             nc.sync.dma_start(out=rows_of(out_0, t), in_=window[t][:])

from contextlib import ExitStack

import concourse.mybir as mybir

K, T, N, U = 512, 512, 512, 1024
FLOPS = 2 * K * N * T

F32 = mybir.dt.float32
BF16 = mybir.dt.bfloat16
I32 = mybir.dt.int32
U32 = mybir.dt.uint32
U16 = mybir.dt.uint16
U8 = mybir.dt.uint8
FP8X4 = mybir.dt.float8_e4m3fn_x4
COPY = mybir.ActivationFunctionType.Copy

P = 128
PACK = 4
LIST = 16
X_ROW = 4
HALF = 256
SPLIT = 544
FIRST = 224
TAKEN = 192
W_CUTS = ((0, 384), (384, 512))
W_SHARE = 72
ON_VECTOR = ((0, 256), (256, SPLIT))
ROUNDED_ON_SCALAR = ((SPLIT, 768), (768, 1024))
LINED_ON_SCALAR = ((SPLIT, 768), (768, 896), (896, 1024))
QUANTISED = ((0, 256), (256, 384), (384, 768), (768, 896), (896, 1024))
STORED = (384, 768, 1024)


def tile_picked_wkvput_none_lo_kernel(tc, x_words, x_scales, mem, w1, slot, out_0, out_1, out_2):
    nc = tc.nc
    with ExitStack() as ctx:
        keep = ctx.enter_context(tc.tile_pool(name="keep", bufs=1))
        psum = ctx.enter_context(tc.psum_pool(name="psum", bufs=1))

        offsets = keep.tile([P, T // LIST], U16, name="offsets")
        planes = keep.tile([P, T], U8, name="planes", align_bytes=64)
        x_codes = keep.tile([P, T], I32, name="x_codes", align_bytes=64)
        w_raw = [keep.tile([P, PACK, c1 - c0], F32, name="w_raw%d" % c0) for c0, c1 in W_CUTS]
        window = [keep.tile([P, U], F32, name="window%d" % t) for t in range(PACK)]

        def rows_of(dram, t):
            return dram.rearrange("(l t) c -> l t c", t=PACK)[:, t, :]

        sc_rows = x_scales[0].bitcast(I32)
        w_rows = w1.rearrange("(p j) c -> p j c", j=PACK)
        x_cols = x_words[0].rearrange("p c r -> p (c r)").bitcast(I32)

        def load_scale_row(queue, r):
            queue.dma_start(out=planes[X_ROW + r : P : 32, :].bitcast(I32), in_=sc_rows[r:16:4, :])

        for r in (0, 1):
            load_scale_row(nc.scalar, r)
        for r, (c0, c1) in enumerate(W_CUTS):
            nc.sync.dma_start(out=w_raw[r][:], in_=w_rows[:, :, c0:c1])
        for r in (2, 3):
            load_scale_row(nc.sync, r)
        nc.sync.dma_start(out=x_codes[:, :HALF], in_=x_cols[:, :HALF])
        nc.sync.dma_start(out=window[0][:], in_=rows_of(mem, 0))
        nc.sync.dma_start(offsets[:], slot)
        nc.sync.dma_start(out=x_codes[:, HALF:], in_=x_cols[:, HALF:])
        for t in (1, 3, 2):
            nc.sync.dma_start(out=window[t][:], in_=rows_of(mem, t))

        w_codes = keep.tile([P, N], I32, name="w_codes", align_bytes=64)
        grouped = [keep.tile([P, 2, P, PACK], BF16, name="grouped%d" % u, align_bytes=64) for u in range(2)]

        def deal(copy, load, u, l0, l1):
            at = W_CUTS[load][0] // PACK
            src = w_raw[load][:].rearrange("p j (l t) -> p l j t", t=PACK)[:, l0 - at : l1 - at, :, 2 * u : 2 * u + 2]
            copy(out=grouped[u][:, :, l0:l1, :].rearrange("p e l j -> p l j e"), in_=src)

        early = W_CUTS[0][1] // PACK
        deal(nc.vector.tensor_copy, 0, 0, 0, early)
        deal(nc.scalar.copy, 0, 1, 0, W_SHARE)
        deal(nc.vector.tensor_copy, 0, 1, W_SHARE, early)
        late = (early + P) // 2
        deal(nc.vector.tensor_copy, 1, 0, early, late)
        deal(nc.scalar.copy, 1, 0, late, P)
        deal(nc.scalar.copy, 1, 1, early, P)
        for t, l0, l1 in [(0, 0, P // 2), (0, P // 2, P)] + [(t, 0, P) for t in range(1, PACK)]:
            cols = slice(t * P + l0, t * P + l1)
            nc.vector.quantize_mx(out=w_codes[:, cols].bitcast(FP8X4), scales=planes[:, cols],
                                  in_=grouped[t // 2][:, t % 2, l0:l1].rearrange("p l j -> p (l j)"))

        def values(name, pieces, copy, out):
            acc = psum.tile([P, sum(c1 - c0 for t, c0, c1 in pieces)], F32, name=name)
            at = 0
            for t, c0, c1 in pieces:
                rows = slice(t * P, (t + 1) * P)
                nc.tensor.matmul_mx(out=acc[:, at : at + c1 - c0], lhsT=w_codes[:, rows].bitcast(FP8X4), lhsT_scale=planes[:, rows],
                                    rhs=x_codes[:, c0:c1].bitcast(FP8X4), rhs_scale=planes[X_ROW:, c0:c1],
                                    start=True, stop=True)
                at = at + c1 - c0
            copy(out=out, in_=acc[:])

        def placed(t, c0, c1):
            return window[t][:].indirect(offsets[:, c0 // LIST : c1 // LIST])

        def scatter_on_vector(t, c0, c1, source):
            nc.vector.tensor_copy(placed(t, c0, c1), source)

        def scatter_on_scalar(t, c0, c1, source):
            nc.scalar.activation(placed(t, c0, c1), source, COPY)

        def round_on_gpsimd(out, in_):
            nc.gpsimd.tensor_scalar(out=out, in0=in_, scalar1=1.0, scalar2=-0.0, op0=mybir.AluOpType.mult, op1=mybir.AluOpType.add)

        pairs = keep.tile([P, 2 * U], F32, name="pairs")
        lined = keep.tile([P, U * PACK], BF16, name="lined", align_bytes=64)

        def round_place(copy, t, c0, c1):
            places = pairs[:].bitcast(BF16).rearrange("p (u c e) -> p u c e", u=2, e=2)
            copy(out=places[:, t // 2, c0:c1, t % 2], in_=window[t][:, c0:c1])

        def line_up(copy, kind, c0, c1):
            words = pairs[:].bitcast(kind).rearrange("p (u c) -> p u c", u=2)[:, :, c0:c1]
            copy(out=lined[:].bitcast(kind).rearrange("p (c u) -> p c u", u=2)[:, c0:c1], in_=words.rearrange("p u c -> p c u"))

        held = [keep.tile([P, T], F32, name="y%d" % t) for t in range(2)]
        y = [held[0][:], held[1][:], pairs[:, U : U + T], pairs[:, U + T :]]

        def half(t, h):
            values("acc%d_%d" % (t, h), ((t, h * HALF, (h + 1) * HALF),), nc.scalar.copy, y[t][:, h * HALF : (h + 1) * HALF])

        for c0, copy in ((0, nc.vector.tensor_copy), (P, nc.scalar.copy)):
            values("first%d" % c0, ((0, c0, c0 + P),), copy, y[0][:, c0 : c0 + P])
        scatter_on_vector(0, 0, FIRST, y[0][:, :FIRST])
        half(1, 0)
        scatter_on_vector(1, 0, HALF, y[1][:, :HALF])
        half(3, 0)
        half(2, 0)
        for t in range(3):
            half(t, 1)
        for c0 in (0, P):
            values("first%d" % c0, ((3, HALF + c0, HALF + c0 + P),), nc.scalar.copy, y[3][:, HALF + c0 : HALF + c0 + P])
        scatter_on_scalar(0, FIRST, T, y[0][:, FIRST:])
        scatter_on_scalar(1, HALF, T, y[1][:, HALF:])
        for t in range(2):
            nc.sync.dma_start(out=rows_of(out_0, t), in_=window[t][:])
            round_place(round_on_gpsimd, t, 0, U)
        scatter_on_vector(3, 0, TAKEN, y[3][:, :TAKEN])
        scatter_on_scalar(3, TAKEN, T, y[3][:, TAKEN:])
        scatter_on_vector(2, 0, T, y[2])
        for t in (3, 2):
            nc.sync.dma_start(out=rows_of(out_0, t), in_=window[t][:])
        round_place(nc.vector.tensor_copy, 3, 0, SPLIT)
        for c0, c1 in ON_VECTOR:
            round_place(nc.vector.tensor_copy, 2, c0, c1)
        for c0, c1 in ON_VECTOR:
            line_up(nc.vector.tensor_copy, I32, c0, c1)
        round_place(nc.scalar.copy, 3, SPLIT, U)
        for c0, c1 in ROUNDED_ON_SCALAR:
            round_place(nc.scalar.copy, 2, c0, c1)
        for c0, c1 in LINED_ON_SCALAR:
            line_up(nc.scalar.copy, U32, c0, c1)

        o_sc = keep.tile([P, U], U8, name="o_sc", align_bytes=64)
        o_codes = keep.tile([P, U], I32, name="o_codes", align_bytes=64)
        o_words = out_1[0].rearrange("p c r -> p (c r)").bitcast(I32)
        stored = 0
        for c0, c1 in QUANTISED:
            nc.vector.quantize_mx(out=o_codes[:, c0:c1].bitcast(FP8X4), scales=o_sc[:, c0:c1], in_=lined[:, c0 * PACK : c1 * PACK])
            if c1 in STORED:
                nc.sync.dma_start(out=o_words[:, stored:c1], in_=o_codes[:, stored:c1])
                stored = c1
        o_rows = out_2[0].bitcast(I32)
        for r in range(4):
            queue = nc.sync if r < 2 else nc.scalar
            queue.dma_start(out=o_rows[r:16:4, :], in_=o_sc[r:P:32, :].bitcast(I32))
